import numpy as np
import ml_dtypes


def mxq(x, axis, fmt="e4m3"):
    dtype, down = {"e4m3": (ml_dtypes.float8_e4m3fn, 7), "e5m2": (ml_dtypes.float8_e5m2, 14)}[fmt]
    v = np.moveaxis(np.asarray(x, np.float32).astype(ml_dtypes.bfloat16).astype(np.float64), axis, -1)
    blocks = v.reshape(v.shape[:-1] + (-1, 32))
    amax = np.abs(blocks).max(-1, keepdims=True)
    byte = np.maximum(np.where(amax > 0, np.frexp(amax)[1] - 1 + 127, 0) - down, 1)
    scale = np.exp2(byte - 127.0)
    codes = (blocks / scale).astype(np.float32).astype(dtype).astype(np.float64)
    return np.moveaxis((codes * scale).reshape(v.shape), -1, axis)


WIDE = False


def mx_kscale(k):
    if not WIDE:
        return np.ones(k)
    levels = np.array([10, -10, 5, -5, 0])
    if k % 512:
        return np.exp2(np.random.permutation(np.resize(levels, k // 32))).repeat(32)
    a = np.empty((k // 512, 16))
    for p in range(k // 512):
        a[p, :8] = np.random.permutation(np.resize(levels, 8))
        for g in range(8):
            far = levels[np.abs(levels - a[p, g]) >= 10]
            a[p, g + 8] = far[np.random.randint(len(far))]
    return np.exp2(a.ravel()).repeat(32)


def f64(x):
    return np.asarray(x).astype(np.float64)


def striped(idx):
    return np.tile(idx.reshape(-1, 16).T, (8, 1)).astype(np.uint16)


def unstriped(offs):
    return offs[:16].T.reshape(-1).astype(np.int64)


def pack_weight(w):
    k, n = w.shape
    w = f64(np.asarray(w, np.float32).astype(ml_dtypes.bfloat16)).reshape(k // 32, 32, n)
    amax = np.abs(w).max(1)
    byte = np.clip(np.where(amax > 0, np.frexp(amax)[1] - 1 + 127 - 7, 1), 1, 254)
    scaled = (w * np.exp2(127.0 - byte)[:, None, :]).reshape(k, n).astype(np.float32)
    words = np.ascontiguousarray(scaled.reshape(k // 512, 128, 4, n).transpose(0, 1, 3, 2)).astype(ml_dtypes.float8_e4m3fn).view(np.uint8)
    return words, np.ascontiguousarray(byte.astype(np.uint8).reshape(k // 512, 16, n))


def unpack_weight(words, scales):
    g, p, n, _ = words.shape
    vals = np.ascontiguousarray(words).view(ml_dtypes.float8_e4m3fn).astype(np.float64) * np.repeat(np.exp2(scales.astype(np.float64) - 127.0), 8, axis=1)[..., None]
    return vals.transpose(0, 1, 3, 2).reshape(g * 512, n)


def relu(v):
    return np.maximum(v, 0.0)


K, T, S, H, N = 1024, 2048, 1024, 512, 128
P = 2 ** 7


def setup_inputs():
    n = np.random.standard_normal
    s = mx_kscale(K)[:, None]
    u = mx_kscale(H)
    packed_xT = pack_weight(n((K, T)) * s)
    packed_w2 = pack_weight(n((H, N)) / np.sqrt(H) / u[:, None])
    return {
        "x_words": packed_xT[0],
        "x_scales": packed_xT[1],
        "w1": (n((K, H)) / np.sqrt(K) / s * u).astype(np.float32),
        "w2_words": packed_w2[0],
        "w2_scales": packed_w2[1],
        "share": np.tile(np.random.uniform(0.1, 0.9, S), (P, 1)).astype(np.float32),
        "offs": striped(np.random.permutation(T)[:S]),
        "par": striped(np.random.permutation(S)[(S * np.random.uniform(0, 1, S) ** 4).astype(np.int64)]),
    }


def reference(x_words, x_scales, w1, w2_words, w2_scales, share, offs, par):
    xq = unpack_weight(x_words, x_scales)[:, unstriped(offs)]
    h = relu(mxq(f64(w1), 0, "e4m3").T @ xq)
    z = h + h[:, unstriped(par)] * f64(share)[:1]
    return unpack_weight(w2_words, w2_scales).T @ mxq(z, 0, "e4m3")

@@ -1,0 +1,232 @@
+from contextlib import ExitStack
+
+import concourse.mybir as mybir
+from concourse.masks import make_identity
+
+K, T, S, H, N = 1024, 2048, 1024, 512, 128
+FLOPS = 2 * K * H * S + 2 * H * N * S
+
+F32 = mybir.dt.float32
+BF16 = mybir.dt.bfloat16
+I32 = mybir.dt.int32
+U32 = mybir.dt.uint32
+U16 = mybir.dt.uint16
+U8 = mybir.dt.uint8
+FP8X4 = mybir.dt.float8_e4m3fn_x4
+MULT = mybir.AluOpType.mult
+ADD = mybir.AluOpType.add
+RELU = mybir.ActivationFunctionType.Relu
+
+P = 128
+PACK = 4
+PASSES = K // (P * PACK)
+BANK = 512
+BLK = 128
+PIECES = ((0, 512, True), (512, 256, True), (768, 256, False))
+
+
+def tile_picked_treeup_relu_p_kernel(tc, x_words, x_scales, w1, w2_words, w2_scales, share, offs, par, out):
+    nc = tc.nc
+    with ExitStack() as ctx:
+        keep = ctx.enter_context(tc.tile_pool(name="keep", bufs=1))
+        psum = ctx.enter_context(tc.psum_pool(name="psum", bufs=1))
+
+        def bank(b, name):
+            return psum.tile([P, BANK], F32, name=name, tag="bank%d" % b)
+
+        offs_sb = keep.tile([P, S // 16], U16, name="offs_sb")
+        par_sb = keep.tile([P, S // 16], U16, name="par_sb")
+        xw = [keep.tile([P, T], U32, name="xw%d" % z, align_bytes=64) for z in range(PASSES)]
+        xs = keep.tile([P, T], U8, name="xs", align_bytes=64)
+        w1_raw = [keep.tile([P, PACK, H], F32, name="w1raw%d" % z, align_bytes=64) for z in range(PASSES)]
+        share_sb = [
+            keep.tile([P, n], F32, name="share%d" % i, tag="chain%d" % i, align_bytes=64)
+            for i, (j0, n, turned) in enumerate(PIECES)
+        ]
+        w2w = keep.tile([P, N], U32, name="w2w", align_bytes=64)
+        w2s = keep.tile([P, N], U8, name="w2s", align_bytes=64)
+        ident = keep.tile([P, P], F32, name="ident", align_bytes=64)
+
+        nc.gpsimd.memset(xs[:].bitcast(I32), 0)
+        nc.vector.memset(w2s[:].bitcast(I32), 0)
+        make_identity(nc, ident[:])
+
+        def load_x(z):
+            nc.sync.dma_start(out=xw[z][:].bitcast(I32), in_=x_words[z].rearrange("p c r -> p (c r)").bitcast(I32))
+
+        def load_w1(z):
+            rows = w1[z * P * PACK : (z + 1) * P * PACK, :]
+            nc.sync.dma_start(out=w1_raw[z][:], in_=rows.rearrange("(p j) c -> p j c", j=PACK))
+
+        nc.sync.dma_start(offs_sb[:], offs)
+        nc.sync.dma_start(par_sb[:], par)
+        nc.sync.dma_start(out=w2w[:].bitcast(I32), in_=w2_words[0].rearrange("p c r -> p (c r)").bitcast(I32))
+        for q in range(4):
+            nc.sync.dma_start(
+                out=xs[32 * q : 32 * q + 4 * PASSES, :].bitcast(I32),
+                in_=x_scales[:, 4 * q : 4 * q + 4, :].bitcast(I32),
+            )
+        load_x(0)
+        load_w1(0)
+        load_x(1)
+        load_w1(1)
+        for i, (j0, n, turned) in enumerate(PIECES):
+            nc.sync.dma_start(out=share_sb[i][:], in_=share[:, j0 : j0 + n])
+        for q in range(4):
+            nc.sync.dma_start(
+                out=w2s[32 * q : 32 * q + 4, :].bitcast(I32),
+                in_=w2_scales[0, 4 * q : 4 * q + 4, :].bitcast(I32),
+            )
+
+        xsg = keep.tile([P, S], U8, name="xsg", align_bytes=64)
+        xg = [keep.tile([P, S], U32, name="xg%d" % z, align_bytes=64) for z in range(PASSES)]
+        w1_codes = {}
+        w1_scales = {}
+        w1_bf = {}
+
+        def cast_w1(z, u, copy):
+            grouped = keep.tile([P, 2, P, PACK], BF16, name="w1bf%d%d" % (z, u), align_bytes=64)
+            src = w1_raw[z][:].rearrange("p j (m t) -> p m j t", t=PACK)[:, :, :, 2 * u : 2 * u + 2]
+            copy(out=grouped[:].rearrange("p e m j -> p m j e"), in_=src)
+            w1_bf[(z, u)] = grouped
+
+        def quant_w1(z, u):
+            codes = keep.tile([P, 2 * P], U32, name="w1c%d%d" % (z, u), align_bytes=64)
+            scales = keep.tile([P, 2 * P], U8, name="w1s%d%d" % (z, u), align_bytes=64)
+            nc.vector.quantize_mx(
+                out=codes[:].bitcast(FP8X4), scales=scales[:], in_=w1_bf[(z, u)][:].rearrange("p e m j -> p (e m j)")
+            )
+            w1_codes[(z, u)] = codes
+            w1_scales[(z, u)] = scales
+
+        h_acc = [[bank(2 * t + a, "hacc%d%d" % (t, a)) for a in range(2)] for t in range(PACK)]
+
+        def first_product(z, t):
+            u, e = divmod(t, 2)
+            for a in range(2):
+                cols = slice(a * BANK, (a + 1) * BANK)
+                nc.tensor.matmul_mx(
+                    out=h_acc[t][a][:],
+                    lhsT=w1_codes[(z, u)][:, e * P : (e + 1) * P].bitcast(FP8X4),
+                    lhsT_scale=w1_scales[(z, u)][:, e * P : (e + 1) * P],
+                    rhs=xg[z][:, cols].bitcast(FP8X4),
+                    rhs_scale=xsg[4 * z : P, cols],
+                    start=(z == 0),
+                    stop=(z == PASSES - 1),
+                )
+
+        nc.vector.tensor_copy(out=xsg[:], in_=xs[:].indirect(offs_sb[:]))
+        nc.vector.tensor_copy(out=xg[0][:], in_=xw[0][:].indirect(offs_sb[:]))
+        cast_w1(0, 0, nc.vector.tensor_copy)
+        cast_w1(0, 1, nc.scalar.copy)
+        quant_w1(0, 0)
+        quant_w1(0, 1)
+        for t in range(PACK):
+            first_product(0, t)
+        nc.vector.tensor_copy(out=xg[1][:], in_=xw[1][:].indirect(offs_sb[:]))
+        cast_w1(1, 0, nc.vector.tensor_copy)
+        cast_w1(1, 1, nc.scalar.copy)
+        quant_w1(1, 0)
+        quant_w1(1, 1)
+
+        h = [keep.tile([P, S], F32, name="h%d" % t, align_bytes=64) for t in range(PACK)]
+        for t in range(PACK):
+            first_product(1, t)
+            nc.scalar.activation(out=h[t][:, 0:BANK], in_=h_acc[t][0][:], func=RELU)
+            if t == 0:
+                nc.vector.tensor_scalar_max(out=h[t][:, BANK:S], in0=h_acc[t][1][:], scalar1=0.0)
+            else:
+                nc.scalar.activation(out=h[t][:, BANK:S], in_=h_acc[t][1][:], func=RELU)
+
+        def second_product(z_in, j0, n, acc):
+            codes = keep.tile([P, n], U32, name="zc%d" % j0, align_bytes=64)
+            scales = keep.tile([P, n], U8, name="zs%d" % j0, align_bytes=64)
+            nc.vector.quantize_mx(out=codes[:].bitcast(FP8X4), scales=scales[:], in_=z_in)
+            nc.tensor.matmul_mx(
+                out=acc,
+                lhsT=w2w[:].bitcast(FP8X4),
+                lhsT_scale=w2s[:],
+                rhs=codes[:].bitcast(FP8X4),
+                rhs_scale=scales[:],
+                start=True,
+                stop=True,
+            )
+
+        def store(j0, n, acc):
+            res = keep.tile([P, n], F32, name="res%d" % j0, align_bytes=64)
+            nc.scalar.copy(out=res[:], in_=acc)
+            nc.sync.dma_start(out=out[:, j0 : j0 + n], in_=res[:])
+
+        def finish(z_in, j0, n):
+            acc = bank(1 + j0 // (2 * BLK), "oacc%d" % j0)
+            second_product(z_in, j0, n, acc[:, 0:n])
+            store(j0, n, acc[:, 0:n])
+
+        later = []
+        for i, (j0, n, turned) in enumerate(PIECES):
+            taken = keep.tile([P, PACK, n], F32, name="taken%d" % j0, tag="chain%d" % (i - 1), align_bytes=64)
+            blocks = n // BLK
+            if turned:
+                z_t = [bank(j0 // BLK + b, "zt%d_%d" % (j0, b)) for b in range(blocks)]
+            else:
+                own = keep.tile([P, PACK, n], F32, name="own%d" % j0, align_bytes=64)
+                for t in range(PACK):
+                    nc.sync.dma_start(out=own[:, t, :], in_=h[t][:, j0 : j0 + n])
+            for t in range(PACK):
+                if turned:
+                    for b in range(blocks):
+                        c0 = j0 + b * BLK
+                        nc.tensor.matmul(
+                            out=z_t[b][:, t * P : (t + 1) * P], lhsT=h[t][:, c0 : c0 + BLK], rhs=ident[:], start=True, stop=False, is_transpose=True
+                        )
+                nc.vector.tensor_tensor(
+                    out=taken[:, t, :],
+                    in0=h[t][:].indirect(par_sb[:, j0 // 16 : (j0 + n) // 16]),
+                    in1=share_sb[i][:],
+                    op=MULT,
+                )
+                if turned:
+                    for b in range(blocks):
+                        dst = z_t[b][:, t * P : (t + 1) * P]
+                        c0 = b * BLK
+                        nc.tensor.matmul(
+                            out=dst, lhsT=taken[:, t, c0 : c0 + BLK], rhs=ident[:], start=False, stop=True, is_transpose=True
+                        )
+            if turned:
+                for pair in range(blocks // 2):
+                    jp = j0 + pair * 2 * BLK
+                    back = bank((6 + jp // (2 * BLK)) % 8, "back%d" % jp)
+                    for b in range(2):
+                        z_rows = keep.tile([P, H], BF16, name="zrows%d_%d" % (jp, b), align_bytes=64)
+                        nc.scalar.copy(
+                            out=z_rows[:].rearrange("p (u m e) -> p u m e", u=2, e=2),
+                            in_=z_t[2 * pair + b][:].rearrange("p (u e m) -> p u m e", u=2, e=2),
+                        )
+                        words = z_rows[:].bitcast(F32)
+                        for u in range(2):
+                            c0 = (2 * b + u) * P
+                            nc.tensor.transpose(back[:, c0 : c0 + P], words[:, u * P : (u + 1) * P], ident[:])
+                    z_in = keep.tile([P, 2 * BLK * PACK], BF16, name="zin%d" % jp, align_bytes=64)
+                    nc.scalar.copy(
+                        out=z_in[:].bitcast(F32).rearrange("p (b j u) -> p b j u", b=2, u=2),
+                        in_=back[:].rearrange("p (b u j) -> p b j u", b=2, u=2),
+                    )
+                    later.append((z_in[:], jp, 2 * BLK))
+            else:
+                for job in later:
+                    finish(*job)
+                z_ins = []
+                for b in range(blocks):
+                    cols = slice(b * BLK, (b + 1) * BLK)
+                    z_in = keep.tile([P, BLK * PACK], BF16, name="zin%d" % (j0 + b * BLK), align_bytes=64)
+                    nc.vector.tensor_tensor(
+                        out=z_in[:].rearrange("p (c i t) -> p c t i", i=4, t=PACK),
+                        in0=own[:, :, cols].rearrange("p t (c i) -> p c t i", i=4),
+                        in1=taken[:, :, cols].rearrange("p t (c i) -> p c t i", i=4),
+                        op=ADD,
+                    )
+                    z_ins.append(z_in)
+                for b in range(blocks):
+                    acc = bank(4 + b, "oacc%d" % (j0 + b * BLK))
+                    second_product(z_ins[b][:], j0 + b * BLK, BLK, acc[:, 0:BLK])
+                    store(j0 + b * BLK, BLK, acc[:, 0:BLK])

@@ -79,15 +79,20 @@ def tile_picked_treeup_relu_p_kernel(tc, x_words, x_scales, w1, w2_words, w2_sca
             )
 
         xsg = keep.tile([P, S], U8, name="xsg", align_bytes=64)
-        xg = [keep.tile([P, S], U32, name="xg%d" % z, align_bytes=64) for z in range(PASSES)]
+        xg = [keep.tile([P, S], U32, name="xg0", align_bytes=64)]
         w1_codes = {}
         w1_scales = {}
         w1_bf = {}
 
-        def cast_w1(z, u, copy):
-            grouped = keep.tile([P, 2, P, PACK], BF16, name="w1bf%d%d" % (z, u), align_bytes=64)
+        def cast_w1(z, u, scalar_m):
+            grouped = keep.tile([P, 2, P, PACK], BF16, name="w1bf%d%d" % (z, u), tag="w1bf%d%d" % (z, u), align_bytes=64)
             src = w1_raw[z][:].rearrange("p j (m t) -> p m j t", t=PACK)[:, :, :, 2 * u : 2 * u + 2]
-            copy(out=grouped[:].rearrange("p e m j -> p m j e"), in_=src)
+            dst = grouped[:].rearrange("p e m j -> p m j e")
+            if scalar_m > 0:
+                nc.scalar.copy(out=dst[:, 0:scalar_m], in_=src[:, 0:scalar_m])
+            for m0 in range(scalar_m, P, P // 2):
+                m1 = min(m0 + P // 2, P)
+                nc.vector.tensor_copy(out=dst[:, m0:m1], in_=src[:, m0:m1])
             w1_bf[(z, u)] = grouped
 
         def quant_w1(z, u):
@@ -117,16 +122,17 @@ def tile_picked_treeup_relu_p_kernel(tc, x_words, x_scales, w1, w2_words, w2_sca
 
         nc.vector.tensor_copy(out=xsg[:], in_=xs[:].indirect(offs_sb[:]))
         nc.vector.tensor_copy(out=xg[0][:], in_=xw[0][:].indirect(offs_sb[:]))
-        cast_w1(0, 0, nc.vector.tensor_copy)
-        cast_w1(0, 1, nc.scalar.copy)
+        cast_w1(0, 0, 0)
+        cast_w1(0, 1, P)
         quant_w1(0, 0)
         quant_w1(0, 1)
         for t in range(PACK):
             first_product(0, t)
+        xg.append(keep.tile([P, S], U32, name="xg1", tag="w1bf01", align_bytes=64))
         nc.vector.tensor_copy(out=xg[1][:], in_=xw[1][:].indirect(offs_sb[:]))
-        cast_w1(1, 0, nc.vector.tensor_copy)
-        cast_w1(1, 1, nc.scalar.copy)
+        cast_w1(1, 0, 72)
         quant_w1(1, 0)
+        cast_w1(1, 1, 64)
         quant_w1(1, 1)
 
         h = [keep.tile([P, S], F32, name="h%d" % t, align_bytes=64) for t in range(PACK)]
@@ -139,28 +145,28 @@ def tile_picked_treeup_relu_p_kernel(tc, x_words, x_scales, w1, w2_words, w2_sca
                 nc.scalar.activation(out=h[t][:, BANK:S], in_=h_acc[t][1][:], func=RELU)
 
         def second_product(z_in, j0, n, acc):
-            codes = keep.tile([P, n], U32, name="zc%d" % j0, align_bytes=64)
-            scales = keep.tile([P, n], U8, name="zs%d" % j0, align_bytes=64)
-            nc.vector.quantize_mx(out=codes[:].bitcast(FP8X4), scales=scales[:], in_=z_in)
+            codes = z_codes[:, j0 : j0 + n]
+            scales = z_scales[:, j0 : j0 + n]
+            nc.vector.quantize_mx(out=codes.bitcast(FP8X4), scales=scales, in_=z_in)
             nc.tensor.matmul_mx(
                 out=acc,
                 lhsT=w2w[:].bitcast(FP8X4),
                 lhsT_scale=w2s[:],
-                rhs=codes[:].bitcast(FP8X4),
-                rhs_scale=scales[:],
+                rhs=codes.bitcast(FP8X4),
+                rhs_scale=scales,
                 start=True,
                 stop=True,
             )
 
-        def store(j0, n, acc):
+        def store(j0, n, acc, copy):
             res = keep.tile([P, n], F32, name="res%d" % j0, align_bytes=64)
-            nc.scalar.copy(out=res[:], in_=acc)
+            copy(out=res[:], in_=acc)
             nc.sync.dma_start(out=out[:, j0 : j0 + n], in_=res[:])
 
         def finish(z_in, j0, n):
             acc = bank(1 + j0 // (2 * BLK), "oacc%d" % j0)
             second_product(z_in, j0, n, acc[:, 0:n])
-            store(j0, n, acc[:, 0:n])
+            store(j0, n, acc[:, 0:n], nc.scalar.copy)
 
         later = []
         for i, (j0, n, turned) in enumerate(PIECES):
@@ -197,7 +203,7 @@ def tile_picked_treeup_relu_p_kernel(tc, x_words, x_scales, w1, w2_words, w2_sca
                     jp = j0 + pair * 2 * BLK
                     back = bank((6 + jp // (2 * BLK)) % 8, "back%d" % jp)
                     for b in range(2):
-                        z_rows = keep.tile([P, H], BF16, name="zrows%d_%d" % (jp, b), align_bytes=64)
+                        z_rows = keep.tile([P, H], BF16, name="zrows%d_%d" % (jp, b), tag="zrows%d_%d" % (jp, b), align_bytes=64)
                         nc.scalar.copy(
                             out=z_rows[:].rearrange("p (u m e) -> p u m e", u=2, e=2),
                             in_=z_t[2 * pair + b][:].rearrange("p (u e m) -> p u m e", u=2, e=2),
@@ -213,6 +219,8 @@ def tile_picked_treeup_relu_p_kernel(tc, x_words, x_scales, w1, w2_words, w2_sca
                     )
                     later.append((z_in[:], jp, 2 * BLK))
             else:
+                z_codes = keep.tile([P, S], U32, name="z_codes", tag="zrows512_1", align_bytes=64)
+                z_scales = keep.tile([P, S], U8, name="z_scales", align_bytes=64)
                 for job in later:
                     finish(*job)
                 z_ins = []
@@ -229,4 +237,4 @@ def tile_picked_treeup_relu_p_kernel(tc, x_words, x_scales, w1, w2_words, w2_sca
                 for b in range(blocks):
                     acc = bank(4 + b, "oacc%d" % (j0 + b * BLK))
                     second_product(z_ins[b][:], j0 + b * BLK, BLK, acc[:, 0:BLK])
-                    store(j0 + b * BLK, BLK, acc[:, 0:BLK])
+                    store(j0 + b * BLK, BLK, acc[:, 0:BLK], nc.vector.tensor_copy if b == blocks - 1 else nc.scalar.copy)

@@ -58,20 +58,20 @@ def tile_picked_treeup_relu_p_kernel(tc, x_words, x_scales, w1, w2_words, w2_sca
             rows = w1[z * P * PACK : (z + 1) * P * PACK, :]
             nc.sync.dma_start(out=w1_raw[z][:], in_=rows.rearrange("(p j) c -> p j c", j=PACK))
 
+        load_x(0)
         nc.sync.dma_start(offs_sb[:], offs)
-        nc.sync.dma_start(par_sb[:], par)
-        nc.sync.dma_start(out=w2w[:].bitcast(I32), in_=w2_words[0].rearrange("p c r -> p (c r)").bitcast(I32))
         for q in range(4):
             nc.sync.dma_start(
                 out=xs[32 * q : 32 * q + 4 * PASSES, :].bitcast(I32),
                 in_=x_scales[:, 4 * q : 4 * q + 4, :].bitcast(I32),
             )
-        load_x(0)
         load_w1(0)
         load_x(1)
         load_w1(1)
+        nc.sync.dma_start(par_sb[:], par)
         for i, (j0, n, turned) in enumerate(PIECES):
             nc.sync.dma_start(out=share_sb[i][:], in_=share[:, j0 : j0 + n])
+        nc.sync.dma_start(out=w2w[:].bitcast(I32), in_=w2_words[0].rearrange("p c r -> p (c r)").bitcast(I32))
         for q in range(4):
             nc.sync.dma_start(
                 out=w2s[32 * q : 32 * q + 4, :].bitcast(I32),
@@ -120,9 +120,9 @@ def tile_picked_treeup_relu_p_kernel(tc, x_words, x_scales, w1, w2_words, w2_sca
                     stop=(z == PASSES - 1),
                 )
 
-        nc.vector.tensor_copy(out=xsg[:], in_=xs[:].indirect(offs_sb[:]))
         nc.vector.tensor_copy(out=xg[0][:], in_=xw[0][:].indirect(offs_sb[:]))
-        cast_w1(0, 0, 0)
+        nc.vector.tensor_copy(out=xsg[:], in_=xs[:].indirect(offs_sb[:]))
+        cast_w1(0, 0, 72)
         cast_w1(0, 1, P)
         quant_w1(0, 0)
         quant_w1(0, 1)
@@ -130,7 +130,7 @@ def tile_picked_treeup_relu_p_kernel(tc, x_words, x_scales, w1, w2_words, w2_sca
             first_product(0, t)
         xg.append(keep.tile([P, S], U32, name="xg1", tag="w1bf01", align_bytes=64))
         nc.vector.tensor_copy(out=xg[1][:], in_=xw[1][:].indirect(offs_sb[:]))
-        cast_w1(1, 0, 72)
+        cast_w1(1, 0, 88)
         quant_w1(1, 0)
         cast_w1(1, 1, 64)
         quant_w1(1, 1)
@@ -185,12 +185,14 @@ def tile_picked_treeup_relu_p_kernel(tc, x_words, x_scales, w1, w2_words, w2_sca
                         nc.tensor.matmul(
                             out=z_t[b][:, t * P : (t + 1) * P], lhsT=h[t][:, c0 : c0 + BLK], rhs=ident[:], start=True, stop=False, is_transpose=True
                         )
-                nc.vector.tensor_tensor(
-                    out=taken[:, t, :],
-                    in0=h[t][:].indirect(par_sb[:, j0 // 16 : (j0 + n) // 16]),
-                    in1=share_sb[i][:],
-                    op=MULT,
-                )
+                step = n if t < PACK - 1 else 2 * BLK
+                for c0 in range(0, n, step):
+                    nc.vector.tensor_tensor(
+                        out=taken[:, t, c0 : c0 + step],
+                        in0=h[t][:].indirect(par_sb[:, (j0 + c0) // 16 : (j0 + c0 + step) // 16]),
+                        in1=share_sb[i][:, c0 : c0 + step],
+                        op=MULT,
+                    )
                 if turned:
                     for b in range(blocks):
                         dst = z_t[b][:, t * P : (t + 1) * P]

@@ -22,7 +22,11 @@ PACK = 4
 PASSES = K // (P * PACK)
 BANK = 512
 BLK = 128
+HALF = P // 2
+LEAD = T // 4
 PIECES = ((0, 512, True), (512, 256, True), (768, 256, False))
+TURN_BANKS = (((0, 1), (2, 3)), ((4,), (5,)))
+BACK_BANKS = ((6, 7), (0,))
 
 
 def tile_picked_treeup_relu_p_kernel(tc, x_words, x_scales, w1, w2_words, w2_scales, share, offs, par, out):
@@ -38,7 +42,8 @@ def tile_picked_treeup_relu_p_kernel(tc, x_words, x_scales, w1, w2_words, w2_sca
         par_sb = keep.tile([P, S // 16], U16, name="par_sb")
         xw = [keep.tile([P, T], U32, name="xw%d" % z, align_bytes=64) for z in range(PASSES)]
         xs = keep.tile([P, T], U8, name="xs", align_bytes=64)
-        w1_raw = [keep.tile([P, PACK, H], F32, name="w1raw%d" % z, align_bytes=64) for z in range(PASSES)]
+        w1_first = keep.tile([P, PACK, H], F32, name="w1first", align_bytes=64)
+        w1_second = [keep.tile([P, PACK, H // 2], F32, name="w1second%d" % c, align_bytes=64) for c in range(2)]
         share_sb = [
             keep.tile([P, n], F32, name="share%d" % i, tag="chain%d" % i, align_bytes=64)
             for i, (j0, n, turned) in enumerate(PIECES)
@@ -51,23 +56,24 @@ def tile_picked_treeup_relu_p_kernel(tc, x_words, x_scales, w1, w2_words, w2_sca
         nc.vector.memset(w2s[:].bitcast(I32), 0)
         make_identity(nc, ident[:])
 
-        def load_x(z):
-            nc.sync.dma_start(out=xw[z][:].bitcast(I32), in_=x_words[z].rearrange("p c r -> p (c r)").bitcast(I32))
+        def load_x(z, c0, c1):
+            src = x_words[z].rearrange("p c r -> p (c r)").bitcast(I32)
+            nc.sync.dma_start(out=xw[z][:, c0:c1].bitcast(I32), in_=src[:, c0:c1])
 
-        def load_w1(z):
-            rows = w1[z * P * PACK : (z + 1) * P * PACK, :]
-            nc.sync.dma_start(out=w1_raw[z][:], in_=rows.rearrange("(p j) c -> p j c", j=PACK))
+        w1_rows = [w1[z * P * PACK : (z + 1) * P * PACK, :].rearrange("(p j) c -> p j c", j=PACK) for z in range(PASSES)]
 
-        load_x(0)
         nc.sync.dma_start(offs_sb[:], offs)
+        load_x(0, 0, LEAD)
         for q in range(4):
             nc.sync.dma_start(
                 out=xs[32 * q : 32 * q + 4 * PASSES, :].bitcast(I32),
                 in_=x_scales[:, 4 * q : 4 * q + 4, :].bitcast(I32),
             )
-        load_w1(0)
-        load_x(1)
-        load_w1(1)
+        load_x(0, LEAD, T)
+        nc.sync.dma_start(out=w1_first[:], in_=w1_rows[0])
+        load_x(1, 0, T)
+        for c in range(2):
+            nc.sync.dma_start(out=w1_second[c][:], in_=w1_rows[1][:, :, c * (H // 2) : (c + 1) * (H // 2)])
         nc.sync.dma_start(par_sb[:], par)
         for i, (j0, n, turned) in enumerate(PIECES):
             nc.sync.dma_start(out=share_sb[i][:], in_=share[:, j0 : j0 + n])
@@ -80,29 +86,26 @@ def tile_picked_treeup_relu_p_kernel(tc, x_words, x_scales, w1, w2_words, w2_sca
 
         xsg = keep.tile([P, S], U8, name="xsg", align_bytes=64)
         xg = [keep.tile([P, S], U32, name="xg0", align_bytes=64)]
+        w1_bf = {}
         w1_codes = {}
         w1_scales = {}
-        w1_bf = {}
+        for z in range(PASSES):
+            for u in range(2):
+                w1_bf[(z, u)] = keep.tile([P, 2, P, PACK], BF16, name="w1bf%d%d" % (z, u), tag="w1bf%d%d" % (z, u), align_bytes=64)
+                w1_codes[(z, u)] = keep.tile([P, 2 * P], U32, name="w1c%d%d" % (z, u), align_bytes=64)
+                w1_scales[(z, u)] = keep.tile([P, 2 * P], U8, name="w1s%d%d" % (z, u), align_bytes=64)
 
-        def cast_w1(z, u, scalar_m):
-            grouped = keep.tile([P, 2, P, PACK], BF16, name="w1bf%d%d" % (z, u), tag="w1bf%d%d" % (z, u), align_bytes=64)
-            src = w1_raw[z][:].rearrange("p j (m t) -> p m j t", t=PACK)[:, :, :, 2 * u : 2 * u + 2]
-            dst = grouped[:].rearrange("p e m j -> p m j e")
-            if scalar_m > 0:
-                nc.scalar.copy(out=dst[:, 0:scalar_m], in_=src[:, 0:scalar_m])
-            for m0 in range(scalar_m, P, P // 2):
-                m1 = min(m0 + P // 2, P)
-                nc.vector.tensor_copy(out=dst[:, m0:m1], in_=src[:, m0:m1])
-            w1_bf[(z, u)] = grouped
+        def cast_w1(copy, raw, first, z, u, m0, count):
+            src = raw[:].rearrange("p j (m t) -> p m j t", t=PACK)[:, m0 - first : m0 - first + count, :, 2 * u : 2 * u + 2]
+            dst = w1_bf[(z, u)][:].rearrange("p e m j -> p m j e")
+            copy(out=dst[:, m0 : m0 + count], in_=src)
 
         def quant_w1(z, u):
-            codes = keep.tile([P, 2 * P], U32, name="w1c%d%d" % (z, u), align_bytes=64)
-            scales = keep.tile([P, 2 * P], U8, name="w1s%d%d" % (z, u), align_bytes=64)
             nc.vector.quantize_mx(
-                out=codes[:].bitcast(FP8X4), scales=scales[:], in_=w1_bf[(z, u)][:].rearrange("p e m j -> p (e m j)")
+                out=w1_codes[(z, u)][:].bitcast(FP8X4),
+                scales=w1_scales[(z, u)][:],
+                in_=w1_bf[(z, u)][:].rearrange("p e m j -> p (e m j)"),
             )
-            w1_codes[(z, u)] = codes
-            w1_scales[(z, u)] = scales
 
         h_acc = [[bank(2 * t + a, "hacc%d%d" % (t, a)) for a in range(2)] for t in range(PACK)]
 
@@ -120,19 +123,22 @@ def tile_picked_treeup_relu_p_kernel(tc, x_words, x_scales, w1, w2_words, w2_sca
                     stop=(z == PASSES - 1),
                 )
 
-        nc.vector.tensor_copy(out=xg[0][:], in_=xw[0][:].indirect(offs_sb[:]))
         nc.vector.tensor_copy(out=xsg[:], in_=xs[:].indirect(offs_sb[:]))
-        cast_w1(0, 0, 72)
-        cast_w1(0, 1, P)
+        nc.vector.tensor_copy(out=xg[0][:], in_=xw[0][:].indirect(offs_sb[:]))
+        cast_w1(nc.scalar.copy, w1_first, 0, 0, 0, 0, P)
+        cast_w1(nc.scalar.copy, w1_first, 0, 0, 1, 0, HALF)
+        cast_w1(nc.vector.tensor_copy, w1_first, 0, 0, 1, HALF, HALF)
         quant_w1(0, 0)
         quant_w1(0, 1)
         for t in range(PACK):
             first_product(0, t)
         xg.append(keep.tile([P, S], U32, name="xg1", tag="w1bf01", align_bytes=64))
         nc.vector.tensor_copy(out=xg[1][:], in_=xw[1][:].indirect(offs_sb[:]))
-        cast_w1(1, 0, 88)
+        cast_w1(nc.scalar.copy, w1_second[0], 0, 1, 0, 0, HALF)
+        cast_w1(nc.scalar.copy, w1_second[0], 0, 1, 1, 0, HALF)
+        cast_w1(nc.vector.tensor_copy, w1_second[1], HALF, 1, 0, HALF, HALF)
+        cast_w1(nc.scalar.copy, w1_second[1], HALF, 1, 1, HALF, HALF)
         quant_w1(1, 0)
-        cast_w1(1, 1, 64)
         quant_w1(1, 1)
 
         h = [keep.tile([P, S], F32, name="h%d" % t, align_bytes=64) for t in range(PACK)]
@@ -144,12 +150,88 @@ def tile_picked_treeup_relu_p_kernel(tc, x_words, x_scales, w1, w2_words, w2_sca
             else:
                 nc.scalar.activation(out=h[t][:, BANK:S], in_=h_acc[t][1][:], func=RELU)
 
-        def second_product(z_in, j0, n, acc):
+        def gather(i, t, taken):
+            j0, n, turned = PIECES[i]
+            nc.vector.tensor_tensor(
+                out=taken[:, t, :],
+                in0=h[t][:].indirect(par_sb[:, j0 // 16 : (j0 + n) // 16]),
+                in1=share_sb[i][:],
+                op=MULT,
+            )
+
+        turned_in = []
+        for i, (j0, n, turned) in enumerate(PIECES):
+            taken = keep.tile([P, PACK, n], F32, name="taken%d" % j0, tag="chain%d" % (i - 1), align_bytes=64)
+            if not turned:
+                own = keep.tile([P, PACK, n], F32, name="own%d" % j0, align_bytes=64)
+                for t in range(PACK):
+                    nc.sync.dma_start(out=own[:, t, :], in_=h[t][:, j0 : j0 + n])
+                for t in range(PACK):
+                    gather(i, t, taken)
+                direct = (own, taken, j0, n)
+                continue
+            groups = [list(range(b0, min(b0 + 2, n // BLK))) for b0 in range(0, n // BLK, 2)]
+            back = [bank(BACK_BANKS[i][g], "back%d_%d" % (i, g)) for g in range(len(groups))]
+            for u in range(2):
+                z_t = [bank(TURN_BANKS[i][u][g], "zt%d_%d_%d" % (i, g, u)) for g in range(len(groups))]
+                for e in range(2):
+                    for g, blocks in enumerate(groups):
+                        for s, b in enumerate(blocks):
+                            nc.tensor.matmul(
+                                out=z_t[g][:, (2 * s + e) * P : (2 * s + e + 1) * P],
+                                lhsT=h[2 * u + e][:, j0 + b * BLK : j0 + (b + 1) * BLK],
+                                rhs=ident[:],
+                                start=(e == 0 and s == 0),
+                                stop=False,
+                                is_transpose=True,
+                            )
+                for e in range(2):
+                    gather(i, 2 * u + e, taken)
+                    for g, blocks in enumerate(groups):
+                        for s, b in enumerate(blocks):
+                            nc.tensor.matmul(
+                                out=z_t[g][:, (2 * s + e) * P : (2 * s + e + 1) * P],
+                                lhsT=taken[:, 2 * u + e, b * BLK : (b + 1) * BLK],
+                                rhs=ident[:],
+                                start=False,
+                                stop=(e == 1 and b == blocks[-1]),
+                                is_transpose=True,
+                            )
+                for g, blocks in enumerate(groups):
+                    width = len(blocks) * 2 * P
+                    name = "zrows%d_%d_%d" % (i, g, u)
+                    z_rows = keep.tile([P, width], BF16, name=name, tag=name, align_bytes=64)
+                    nc.scalar.copy(
+                        out=z_rows[:].rearrange("p (s m e) -> p s m e", m=P, e=2),
+                        in_=z_t[g][:, 0:width].rearrange("p (s e m) -> p s m e", m=P, e=2),
+                    )
+                    words = z_rows[:].bitcast(F32)
+                    for s in range(len(blocks)):
+                        c0 = (2 * s + u) * P
+                        nc.tensor.transpose(back[g][:, c0 : c0 + P], words[:, s * P : (s + 1) * P], ident[:])
+            for g, blocks in enumerate(groups):
+                width = len(blocks) * 2 * P
+                if i > 0 or g == 0:
+                    cols = n if i == 0 else len(blocks) * BLK
+                    jz = j0 + blocks[0] * BLK
+                    z_in = keep.tile([P, cols * PACK], BF16, name="zin%d" % jz, tag="zin%d" % jz, align_bytes=64)
+                    turned_in.append((z_in, jz, cols))
+                c0 = (j0 + blocks[0] * BLK - jz) * PACK
+                nc.scalar.copy(
+                    out=z_in[:, c0 : c0 + 2 * width].bitcast(F32).rearrange("p (s j u) -> p s j u", j=BLK, u=2),
+                    in_=back[g][:, 0:width].rearrange("p (s u j) -> p s j u", j=BLK, u=2),
+                )
+
+        z_codes = keep.tile([P, S], U32, name="z_codes", tag="zrows1_0_1", align_bytes=64)
+        z_scales = keep.tile([P, S], U8, name="z_scales", align_bytes=64)
+
+        def finish(z_in, j0, n, b, copy):
             codes = z_codes[:, j0 : j0 + n]
             scales = z_scales[:, j0 : j0 + n]
             nc.vector.quantize_mx(out=codes.bitcast(FP8X4), scales=scales, in_=z_in)
+            acc = bank(b, "oacc%d" % j0)
             nc.tensor.matmul_mx(
-                out=acc,
+                out=acc[:, 0:n],
                 lhsT=w2w[:].bitcast(FP8X4),
                 lhsT_scale=w2s[:],
                 rhs=codes.bitcast(FP8X4),
@@ -157,86 +239,27 @@ def tile_picked_treeup_relu_p_kernel(tc, x_words, x_scales, w1, w2_words, w2_sca
                 start=True,
                 stop=True,
             )
-
-        def store(j0, n, acc, copy):
             res = keep.tile([P, n], F32, name="res%d" % j0, align_bytes=64)
-            copy(out=res[:], in_=acc)
+            copy(out=res[:], in_=acc[:, 0:n])
             nc.sync.dma_start(out=out[:, j0 : j0 + n], in_=res[:])
 
-        def finish(z_in, j0, n):
-            acc = bank(1 + j0 // (2 * BLK), "oacc%d" % j0)
-            second_product(z_in, j0, n, acc[:, 0:n])
-            store(j0, n, acc[:, 0:n], nc.scalar.copy)
+        own, taken, j0, n = direct
+        z_in, jt, nt = turned_in[0]
+        finish(z_in[:], jt, nt, 1, nc.scalar.copy)
+        z_direct = keep.tile([P, 2, BLK * PACK], BF16, name="zdirect", tag="zin0", align_bytes=64)
 
-        later = []
-        for i, (j0, n, turned) in enumerate(PIECES):
-            taken = keep.tile([P, PACK, n], F32, name="taken%d" % j0, tag="chain%d" % (i - 1), align_bytes=64)
-            blocks = n // BLK
-            if turned:
-                z_t = [bank(j0 // BLK + b, "zt%d_%d" % (j0, b)) for b in range(blocks)]
-            else:
-                own = keep.tile([P, PACK, n], F32, name="own%d" % j0, align_bytes=64)
-                for t in range(PACK):
-                    nc.sync.dma_start(out=own[:, t, :], in_=h[t][:, j0 : j0 + n])
-            for t in range(PACK):
-                if turned:
-                    for b in range(blocks):
-                        c0 = j0 + b * BLK
-                        nc.tensor.matmul(
-                            out=z_t[b][:, t * P : (t + 1) * P], lhsT=h[t][:, c0 : c0 + BLK], rhs=ident[:], start=True, stop=False, is_transpose=True
-                        )
-                step = n if t < PACK - 1 else 2 * BLK
-                for c0 in range(0, n, step):
-                    nc.vector.tensor_tensor(
-                        out=taken[:, t, c0 : c0 + step],
-                        in0=h[t][:].indirect(par_sb[:, (j0 + c0) // 16 : (j0 + c0 + step) // 16]),
-                        in1=share_sb[i][:, c0 : c0 + step],
-                        op=MULT,
-                    )
-                if turned:
-                    for b in range(blocks):
-                        dst = z_t[b][:, t * P : (t + 1) * P]
-                        c0 = b * BLK
-                        nc.tensor.matmul(
-                            out=dst, lhsT=taken[:, t, c0 : c0 + BLK], rhs=ident[:], start=False, stop=True, is_transpose=True
-                        )
-            if turned:
-                for pair in range(blocks // 2):
-                    jp = j0 + pair * 2 * BLK
-                    back = bank((6 + jp // (2 * BLK)) % 8, "back%d" % jp)
-                    for b in range(2):
-                        z_rows = keep.tile([P, H], BF16, name="zrows%d_%d" % (jp, b), tag="zrows%d_%d" % (jp, b), align_bytes=64)
-                        nc.scalar.copy(
-                            out=z_rows[:].rearrange("p (u m e) -> p u m e", u=2, e=2),
-                            in_=z_t[2 * pair + b][:].rearrange("p (u e m) -> p u m e", u=2, e=2),
-                        )
-                        words = z_rows[:].bitcast(F32)
-                        for u in range(2):
-                            c0 = (2 * b + u) * P
-                            nc.tensor.transpose(back[:, c0 : c0 + P], words[:, u * P : (u + 1) * P], ident[:])
-                    z_in = keep.tile([P, 2 * BLK * PACK], BF16, name="zin%d" % jp, align_bytes=64)
-                    nc.scalar.copy(
-                        out=z_in[:].bitcast(F32).rearrange("p (b j u) -> p b j u", b=2, u=2),
-                        in_=back[:].rearrange("p (b u j) -> p b j u", b=2, u=2),
-                    )
-                    later.append((z_in[:], jp, 2 * BLK))
-            else:
-                z_codes = keep.tile([P, S], U32, name="z_codes", tag="zrows512_1", align_bytes=64)
-                z_scales = keep.tile([P, S], U8, name="z_scales", align_bytes=64)
-                for job in later:
-                    finish(*job)
-                z_ins = []
-                for b in range(blocks):
-                    cols = slice(b * BLK, (b + 1) * BLK)
-                    z_in = keep.tile([P, BLK * PACK], BF16, name="zin%d" % (j0 + b * BLK), align_bytes=64)
-                    nc.vector.tensor_tensor(
-                        out=z_in[:].rearrange("p (c i t) -> p c t i", i=4, t=PACK),
-                        in0=own[:, :, cols].rearrange("p t (c i) -> p c t i", i=4),
-                        in1=taken[:, :, cols].rearrange("p t (c i) -> p c t i", i=4),
-                        op=ADD,
-                    )
-                    z_ins.append(z_in)
-                for b in range(blocks):
-                    acc = bank(4 + b, "oacc%d" % (j0 + b * BLK))
-                    second_product(z_ins[b][:], j0 + b * BLK, BLK, acc[:, 0:BLK])
-                    store(j0 + b * BLK, BLK, acc[:, 0:BLK], nc.vector.tensor_copy if b == blocks - 1 else nc.scalar.copy)
+        def add_direct(b):
+            cols = slice(b * BLK, (b + 1) * BLK)
+            nc.vector.tensor_tensor(
+                out=z_direct[:, b, :].rearrange("p (c i t) -> p c t i", i=4, t=PACK),
+                in0=own[:, :, cols].rearrange("p t (c i) -> p c t i", i=4),
+                in1=taken[:, :, cols].rearrange("p t (c i) -> p c t i", i=4),
+                op=ADD,
+            )
+
+        add_direct(0)
+        z_in, jt, nt = turned_in[1]
+        finish(z_in[:], jt, nt, 2, nc.scalar.copy)
+        add_direct(1)
+        finish(z_direct[:, 0, :], j0, BLK, 3, nc.scalar.copy)
+        finish(z_direct[:, 1, :], j0 + BLK, BLK, 4, nc.vector.tensor_copy)

@@ -42,8 +42,7 @@ def tile_picked_treeup_relu_p_kernel(tc, x_words, x_scales, w1, w2_words, w2_sca
         par_sb = keep.tile([P, S // 16], U16, name="par_sb")
         xw = [keep.tile([P, T], U32, name="xw%d" % z, align_bytes=64) for z in range(PASSES)]
         xs = keep.tile([P, T], U8, name="xs", align_bytes=64)
-        w1_first = keep.tile([P, PACK, H], F32, name="w1first", align_bytes=64)
-        w1_second = [keep.tile([P, PACK, H // 2], F32, name="w1second%d" % c, align_bytes=64) for c in range(2)]
+        w1_raw = [keep.tile([P, PACK, H], F32, name="w1raw%d" % z, align_bytes=64) for z in range(PASSES)]
         share_sb = [
             keep.tile([P, n], F32, name="share%d" % i, tag="chain%d" % i, align_bytes=64)
             for i, (j0, n, turned) in enumerate(PIECES)
@@ -70,10 +69,9 @@ def tile_picked_treeup_relu_p_kernel(tc, x_words, x_scales, w1, w2_words, w2_sca
                 in_=x_scales[:, 4 * q : 4 * q + 4, :].bitcast(I32),
             )
         load_x(0, LEAD, T)
-        nc.sync.dma_start(out=w1_first[:], in_=w1_rows[0])
+        nc.sync.dma_start(out=w1_raw[0][:], in_=w1_rows[0])
         load_x(1, 0, T)
-        for c in range(2):
-            nc.sync.dma_start(out=w1_second[c][:], in_=w1_rows[1][:, :, c * (H // 2) : (c + 1) * (H // 2)])
+        nc.sync.dma_start(out=w1_raw[1][:], in_=w1_rows[1])
         nc.sync.dma_start(par_sb[:], par)
         for i, (j0, n, turned) in enumerate(PIECES):
             nc.sync.dma_start(out=share_sb[i][:], in_=share[:, j0 : j0 + n])
@@ -95,16 +93,16 @@ def tile_picked_treeup_relu_p_kernel(tc, x_words, x_scales, w1, w2_words, w2_sca
                 w1_codes[(z, u)] = keep.tile([P, 2 * P], U32, name="w1c%d%d" % (z, u), align_bytes=64)
                 w1_scales[(z, u)] = keep.tile([P, 2 * P], U8, name="w1s%d%d" % (z, u), align_bytes=64)
 
-        def cast_w1(copy, raw, first, z, u, m0, count):
-            src = raw[:].rearrange("p j (m t) -> p m j t", t=PACK)[:, m0 - first : m0 - first + count, :, 2 * u : 2 * u + 2]
+        def cast_w1(copy, z, u, m0, count):
+            src = w1_raw[z][:].rearrange("p j (m t) -> p m j t", t=PACK)[:, m0 : m0 + count, :, 2 * u : 2 * u + 2]
             dst = w1_bf[(z, u)][:].rearrange("p e m j -> p m j e")
             copy(out=dst[:, m0 : m0 + count], in_=src)
 
-        def quant_w1(z, u):
+        def quant_w1(z, u, e0=0, e1=2):
             nc.vector.quantize_mx(
-                out=w1_codes[(z, u)][:].bitcast(FP8X4),
-                scales=w1_scales[(z, u)][:],
-                in_=w1_bf[(z, u)][:].rearrange("p e m j -> p (e m j)"),
+                out=w1_codes[(z, u)][:, e0 * P : e1 * P].bitcast(FP8X4),
+                scales=w1_scales[(z, u)][:, e0 * P : e1 * P],
+                in_=w1_bf[(z, u)][:, e0:e1].rearrange("p e m j -> p (e m j)"),
             )
 
         h_acc = [[bank(2 * t + a, "hacc%d%d" % (t, a)) for a in range(2)] for t in range(PACK)]
@@ -125,30 +123,32 @@ def tile_picked_treeup_relu_p_kernel(tc, x_words, x_scales, w1, w2_words, w2_sca
 
         nc.vector.tensor_copy(out=xsg[:], in_=xs[:].indirect(offs_sb[:]))
         nc.vector.tensor_copy(out=xg[0][:], in_=xw[0][:].indirect(offs_sb[:]))
-        cast_w1(nc.scalar.copy, w1_first, 0, 0, 0, 0, P)
-        cast_w1(nc.scalar.copy, w1_first, 0, 0, 1, 0, HALF)
-        cast_w1(nc.vector.tensor_copy, w1_first, 0, 0, 1, HALF, HALF)
+        cast_w1(nc.scalar.copy, 0, 0, 0, P)
+        cast_w1(nc.scalar.copy, 0, 1, 0, HALF)
+        cast_w1(nc.vector.tensor_copy, 0, 1, HALF, HALF)
         quant_w1(0, 0)
         quant_w1(0, 1)
         for t in range(PACK):
             first_product(0, t)
         xg.append(keep.tile([P, S], U32, name="xg1", tag="w1bf01", align_bytes=64))
         nc.vector.tensor_copy(out=xg[1][:], in_=xw[1][:].indirect(offs_sb[:]))
-        cast_w1(nc.scalar.copy, w1_second[0], 0, 1, 0, 0, HALF)
-        cast_w1(nc.scalar.copy, w1_second[0], 0, 1, 1, 0, HALF)
-        cast_w1(nc.vector.tensor_copy, w1_second[1], HALF, 1, 0, HALF, HALF)
-        cast_w1(nc.scalar.copy, w1_second[1], HALF, 1, 1, HALF, HALF)
-        quant_w1(1, 0)
-        quant_w1(1, 1)
+        for u in range(2):
+            cast_w1(nc.scalar.copy, 1, u, 0, HALF)
+            cast_w1(nc.vector.tensor_copy, 1, u, HALF, HALF)
+            if u == 0:
+                quant_w1(1, 0, 0, 1)
+                quant_w1(1, 0, 1, 2)
+            else:
+                quant_w1(1, 1)
 
         h = [keep.tile([P, S], F32, name="h%d" % t, align_bytes=64) for t in range(PACK)]
         for t in range(PACK):
             first_product(1, t)
-            nc.scalar.activation(out=h[t][:, 0:BANK], in_=h_acc[t][0][:], func=RELU)
             if t == 0:
-                nc.vector.tensor_scalar_max(out=h[t][:, BANK:S], in0=h_acc[t][1][:], scalar1=0.0)
+                nc.vector.tensor_scalar_max(out=h[t][:, 0:BANK], in0=h_acc[t][0][:], scalar1=0.0)
             else:
-                nc.scalar.activation(out=h[t][:, BANK:S], in_=h_acc[t][1][:], func=RELU)
+                nc.scalar.activation(out=h[t][:, 0:BANK], in_=h_acc[t][0][:], func=RELU)
+            nc.scalar.activation(out=h[t][:, BANK:S], in_=h_acc[t][1][:], func=RELU)
 
         def gather(i, t, taken):
             j0, n, turned = PIECES[i]

@@ -23,7 +23,6 @@ PASSES = K // (P * PACK)
 BANK = 512
 BLK = 128
 HALF = P // 2
-LEAD = T // 4
 PIECES = ((0, 512, True), (512, 256, True), (768, 256, False))
 TURN_BANKS = (((0, 1), (2, 3)), ((4,), (5,)))
 BACK_BANKS = ((6, 7), (0,))
@@ -55,22 +54,20 @@ def tile_picked_treeup_relu_p_kernel(tc, x_words, x_scales, w1, w2_words, w2_sca
         nc.vector.memset(w2s[:].bitcast(I32), 0)
         make_identity(nc, ident[:])
 
-        def load_x(z, c0, c1):
-            src = x_words[z].rearrange("p c r -> p (c r)").bitcast(I32)
-            nc.sync.dma_start(out=xw[z][:, c0:c1].bitcast(I32), in_=src[:, c0:c1])
+        def load_x(z):
+            nc.sync.dma_start(out=xw[z][:].bitcast(I32), in_=x_words[z].rearrange("p c r -> p (c r)").bitcast(I32))
 
         w1_rows = [w1[z * P * PACK : (z + 1) * P * PACK, :].rearrange("(p j) c -> p j c", j=PACK) for z in range(PASSES)]
 
+        load_x(0)
         nc.sync.dma_start(offs_sb[:], offs)
-        load_x(0, 0, LEAD)
         for q in range(4):
             nc.sync.dma_start(
                 out=xs[32 * q : 32 * q + 4 * PASSES, :].bitcast(I32),
                 in_=x_scales[:, 4 * q : 4 * q + 4, :].bitcast(I32),
             )
-        load_x(0, LEAD, T)
         nc.sync.dma_start(out=w1_raw[0][:], in_=w1_rows[0])
-        load_x(1, 0, T)
+        load_x(1)
         nc.sync.dma_start(out=w1_raw[1][:], in_=w1_rows[1])
         nc.sync.dma_start(par_sb[:], par)
         for i, (j0, n, turned) in enumerate(PIECES):
@@ -83,66 +80,73 @@ def tile_picked_treeup_relu_p_kernel(tc, x_words, x_scales, w1, w2_words, w2_sca
             )
 
         xsg = keep.tile([P, S], U8, name="xsg", align_bytes=64)
-        xg = [keep.tile([P, S], U32, name="xg0", align_bytes=64)]
-        w1_bf = {}
-        w1_codes = {}
-        w1_scales = {}
-        for z in range(PASSES):
-            for u in range(2):
-                w1_bf[(z, u)] = keep.tile([P, 2, P, PACK], BF16, name="w1bf%d%d" % (z, u), tag="w1bf%d%d" % (z, u), align_bytes=64)
-                w1_codes[(z, u)] = keep.tile([P, 2 * P], U32, name="w1c%d%d" % (z, u), align_bytes=64)
-                w1_scales[(z, u)] = keep.tile([P, 2 * P], U8, name="w1s%d%d" % (z, u), align_bytes=64)
+        xg0 = keep.tile([P, S], U32, name="xg0", align_bytes=64)
+        xg = {(0, a): xg0[:, a * BANK : (a + 1) * BANK] for a in range(2)}
+        w1_bf = {
+            (z, u): keep.tile([P, 2, P, PACK], BF16, name="w1bf%d%d" % (z, u), tag="w1bf%d%d" % (z, u), align_bytes=64)
+            for z in range(PASSES)
+            for u in range(2)
+        }
+        w1_mx = {}
 
         def cast_w1(copy, z, u, m0, count):
             src = w1_raw[z][:].rearrange("p j (m t) -> p m j t", t=PACK)[:, m0 : m0 + count, :, 2 * u : 2 * u + 2]
             dst = w1_bf[(z, u)][:].rearrange("p e m j -> p m j e")
             copy(out=dst[:, m0 : m0 + count], in_=src)
 
-        def quant_w1(z, u, e0=0, e1=2):
+        def quant_w1(z, t0, planes, tag=None):
+            u, e = divmod(t0, 2)
+            name = "w1c%d%d" % (z, t0)
+            codes = keep.tile([P, planes * P], U32, name=name, tag=tag or name, align_bytes=64)
+            scales = keep.tile([P, planes * P], U8, name="w1s%d%d" % (z, t0), align_bytes=64)
             nc.vector.quantize_mx(
-                out=w1_codes[(z, u)][:, e0 * P : e1 * P].bitcast(FP8X4),
-                scales=w1_scales[(z, u)][:, e0 * P : e1 * P],
-                in_=w1_bf[(z, u)][:, e0:e1].rearrange("p e m j -> p (e m j)"),
+                out=codes[:].bitcast(FP8X4),
+                scales=scales[:],
+                in_=w1_bf[(z, u)][:, e : e + planes].rearrange("p e m j -> p (e m j)"),
             )
+            for i in range(planes):
+                w1_mx[(z, t0 + i)] = (codes[:, i * P : (i + 1) * P], scales[:, i * P : (i + 1) * P])
 
         h_acc = [[bank(2 * t + a, "hacc%d%d" % (t, a)) for a in range(2)] for t in range(PACK)]
 
         def first_product(z, t):
-            u, e = divmod(t, 2)
+            codes, scales = w1_mx[(z, t)]
             for a in range(2):
                 cols = slice(a * BANK, (a + 1) * BANK)
                 nc.tensor.matmul_mx(
                     out=h_acc[t][a][:],
-                    lhsT=w1_codes[(z, u)][:, e * P : (e + 1) * P].bitcast(FP8X4),
-                    lhsT_scale=w1_scales[(z, u)][:, e * P : (e + 1) * P],
-                    rhs=xg[z][:, cols].bitcast(FP8X4),
+                    lhsT=codes.bitcast(FP8X4),
+                    lhsT_scale=scales,
+                    rhs=xg[(z, a)].bitcast(FP8X4),
                     rhs_scale=xsg[4 * z : P, cols],
                     start=(z == 0),
                     stop=(z == PASSES - 1),
                 )
 
+        nc.vector.tensor_copy(out=xg0[:], in_=xw[0][:].indirect(offs_sb[:]))
         nc.vector.tensor_copy(out=xsg[:], in_=xs[:].indirect(offs_sb[:]))
-        nc.vector.tensor_copy(out=xg[0][:], in_=xw[0][:].indirect(offs_sb[:]))
-        cast_w1(nc.scalar.copy, 0, 0, 0, P)
-        cast_w1(nc.scalar.copy, 0, 1, 0, HALF)
-        cast_w1(nc.vector.tensor_copy, 0, 1, HALF, HALF)
-        quant_w1(0, 0)
-        quant_w1(0, 1)
-        for t in range(PACK):
-            first_product(0, t)
-        xg.append(keep.tile([P, S], U32, name="xg1", tag="w1bf01", align_bytes=64))
-        nc.vector.tensor_copy(out=xg[1][:], in_=xw[1][:].indirect(offs_sb[:]))
         for u in range(2):
-            cast_w1(nc.scalar.copy, 1, u, 0, HALF)
-            cast_w1(nc.vector.tensor_copy, 1, u, HALF, HALF)
-            if u == 0:
-                quant_w1(1, 0, 0, 1)
-                quant_w1(1, 0, 1, 2)
-            else:
-                quant_w1(1, 1)
+            cast_w1(nc.scalar.copy, 0, u, 0, P)
+        quant_w1(0, 0, 2)
+        xg1 = keep.tile([P, S], U32, name="xg1", tag="w1bf00", align_bytes=64)
+        nc.vector.tensor_copy(out=xg1[:], in_=xw[1][:].indirect(offs_sb[:]))
+        for a in range(2):
+            xg[(1, a)] = xg1[:, a * BANK : (a + 1) * BANK]
+        for t in range(2):
+            first_product(0, t)
+        cast_w1(nc.scalar.copy, 1, 0, 0, HALF)
+        cast_w1(nc.vector.tensor_copy, 1, 0, HALF, HALF)
+        quant_w1(1, 0, 1)
+        quant_w1(1, 1, 1)
+        cast_w1(nc.scalar.copy, 1, 1, 0, HALF)
+        cast_w1(nc.vector.tensor_copy, 1, 1, HALF, HALF)
+        quant_w1(0, 2, 2, "w1bf10")
+        quant_w1(1, 2, 2)
 
         h = [keep.tile([P, S], F32, name="h%d" % t, align_bytes=64) for t in range(PACK)]
         for t in range(PACK):
+            if t >= 2:
+                first_product(0, t)
             first_product(1, t)
             if t == 0:
                 nc.vector.tensor_scalar_max(out=h[t][:, 0:BANK], in0=h_acc[t][0][:], scalar1=0.0)

@@ -22,10 +22,9 @@ PACK = 4
 PASSES = K // (P * PACK)
 BANK = 512
 BLK = 128
-HALF = P // 2
-PIECES = ((0, 512, True), (512, 256, True), (768, 256, False))
-TURN_BANKS = (((0, 1), (2, 3)), ((4,), (5,)))
-BACK_BANKS = ((6, 7), (0,))
+ROWS = 16
+TURNED = 5 * BLK
+ADDED = S - TURNED
 
 
 def tile_picked_treeup_relu_p_kernel(tc, x_words, x_scales, w1, w2_words, w2_scales, share, offs, par, out):
@@ -34,21 +33,22 @@ def tile_picked_treeup_relu_p_kernel(tc, x_words, x_scales, w1, w2_words, w2_sca
         keep = ctx.enter_context(tc.tile_pool(name="keep", bufs=1))
         psum = ctx.enter_context(tc.psum_pool(name="psum", bufs=1))
 
+        def sb(shape, dtype, name, reuses=None):
+            return keep.tile(shape, dtype, name=name, tag=reuses or name, align_bytes=64)
+
         def bank(b, name):
             return psum.tile([P, BANK], F32, name=name, tag="bank%d" % b)
 
-        offs_sb = keep.tile([P, S // 16], U16, name="offs_sb")
-        par_sb = keep.tile([P, S // 16], U16, name="par_sb")
-        xw = [keep.tile([P, T], U32, name="xw%d" % z, align_bytes=64) for z in range(PASSES)]
-        xs = keep.tile([P, T], U8, name="xs", align_bytes=64)
-        w1_raw = [keep.tile([P, PACK, H], F32, name="w1raw%d" % z, align_bytes=64) for z in range(PASSES)]
-        share_sb = [
-            keep.tile([P, n], F32, name="share%d" % i, tag="chain%d" % i, align_bytes=64)
-            for i, (j0, n, turned) in enumerate(PIECES)
-        ]
-        w2w = keep.tile([P, N], U32, name="w2w", align_bytes=64)
-        w2s = keep.tile([P, N], U8, name="w2s", align_bytes=64)
-        ident = keep.tile([P, P], F32, name="ident", align_bytes=64)
+        offs_sb = keep.tile([P, S // ROWS], U16, name="offs_sb")
+        par_sb = keep.tile([P, S // ROWS], U16, name="par_sb")
+        xw = [sb([P, T], U32, "xw%d" % z) for z in range(PASSES)]
+        xs = sb([P, T], U8, "xs")
+        w1_raw = [sb([P, PACK, H], F32, "w1raw%d" % z) for z in range(PASSES)]
+        share_turned = sb([P, TURNED], F32, "share_turned")
+        share_added = sb([P, ADDED], F32, "share_added")
+        w2w = sb([P, N], U32, "w2w")
+        w2s = sb([P, N], U8, "w2s")
+        ident = sb([P, P], F32, "ident")
 
         nc.gpsimd.memset(xs[:].bitcast(I32), 0)
         nc.vector.memset(w2s[:].bitcast(I32), 0)
@@ -57,7 +57,9 @@ def tile_picked_treeup_relu_p_kernel(tc, x_words, x_scales, w1, w2_words, w2_sca
         def load_x(z):
             nc.sync.dma_start(out=xw[z][:].bitcast(I32), in_=x_words[z].rearrange("p c r -> p (c r)").bitcast(I32))
 
-        w1_rows = [w1[z * P * PACK : (z + 1) * P * PACK, :].rearrange("(p j) c -> p j c", j=PACK) for z in range(PASSES)]
+        def load_w1(z):
+            rows = w1[z * P * PACK : (z + 1) * P * PACK, :]
+            nc.sync.dma_start(out=w1_raw[z][:], in_=rows.rearrange("(p j) c -> p j c", j=PACK))
 
         load_x(0)
         nc.sync.dma_start(offs_sb[:], offs)
@@ -66,12 +68,12 @@ def tile_picked_treeup_relu_p_kernel(tc, x_words, x_scales, w1, w2_words, w2_sca
                 out=xs[32 * q : 32 * q + 4 * PASSES, :].bitcast(I32),
                 in_=x_scales[:, 4 * q : 4 * q + 4, :].bitcast(I32),
             )
-        nc.sync.dma_start(out=w1_raw[0][:], in_=w1_rows[0])
+        load_w1(0)
         load_x(1)
-        nc.sync.dma_start(out=w1_raw[1][:], in_=w1_rows[1])
+        load_w1(1)
         nc.sync.dma_start(par_sb[:], par)
-        for i, (j0, n, turned) in enumerate(PIECES):
-            nc.sync.dma_start(out=share_sb[i][:], in_=share[:, j0 : j0 + n])
+        nc.sync.dma_start(out=share_turned[:], in_=share[:, 0:TURNED])
+        nc.sync.dma_start(out=share_added[:], in_=share[:, TURNED:S])
         nc.sync.dma_start(out=w2w[:].bitcast(I32), in_=w2_words[0].rearrange("p c r -> p (c r)").bitcast(I32))
         for q in range(4):
             nc.sync.dma_start(
@@ -79,26 +81,17 @@ def tile_picked_treeup_relu_p_kernel(tc, x_words, x_scales, w1, w2_words, w2_sca
                 in_=w2_scales[0, 4 * q : 4 * q + 4, :].bitcast(I32),
             )
 
-        xsg = keep.tile([P, S], U8, name="xsg", align_bytes=64)
-        xg0 = keep.tile([P, S], U32, name="xg0", align_bytes=64)
-        xg = {(0, a): xg0[:, a * BANK : (a + 1) * BANK] for a in range(2)}
-        w1_bf = {
-            (z, u): keep.tile([P, 2, P, PACK], BF16, name="w1bf%d%d" % (z, u), tag="w1bf%d%d" % (z, u), align_bytes=64)
-            for z in range(PASSES)
-            for u in range(2)
-        }
+        w1_bf = {(z, u): sb([P, 2, P, PACK], BF16, "w1bf%d%d" % (z, u)) for z in range(PASSES) for u in range(2)}
         w1_mx = {}
 
-        def cast_w1(copy, z, u, m0, count):
-            src = w1_raw[z][:].rearrange("p j (m t) -> p m j t", t=PACK)[:, m0 : m0 + count, :, 2 * u : 2 * u + 2]
-            dst = w1_bf[(z, u)][:].rearrange("p e m j -> p m j e")
-            copy(out=dst[:, m0 : m0 + count], in_=src)
+        def cast_w1(copy, z, u, m0, m1):
+            src = w1_raw[z][:].rearrange("p j (m t) -> p m j t", t=PACK)[:, m0:m1, :, 2 * u : 2 * u + 2]
+            copy(out=w1_bf[(z, u)][:].rearrange("p e m j -> p m j e")[:, m0:m1], in_=src)
 
-        def quant_w1(z, t0, planes, tag=None):
+        def quant_w1(z, t0, planes, reuses=None):
             u, e = divmod(t0, 2)
-            name = "w1c%d%d" % (z, t0)
-            codes = keep.tile([P, planes * P], U32, name=name, tag=tag or name, align_bytes=64)
-            scales = keep.tile([P, planes * P], U8, name="w1s%d%d" % (z, t0), align_bytes=64)
+            codes = sb([P, planes * P], U32, "w1c%d%d" % (z, t0), reuses)
+            scales = sb([P, planes * P], U8, "w1s%d%d" % (z, t0))
             nc.vector.quantize_mx(
                 out=codes[:].bitcast(FP8X4),
                 scales=scales[:],
@@ -107,6 +100,8 @@ def tile_picked_treeup_relu_p_kernel(tc, x_words, x_scales, w1, w2_words, w2_sca
             for i in range(planes):
                 w1_mx[(z, t0 + i)] = (codes[:, i * P : (i + 1) * P], scales[:, i * P : (i + 1) * P])
 
+        xsg = sb([P, S], U8, "xsg")
+        xg = [sb([P, S], U32, "xg0")]
         h_acc = [[bank(2 * t + a, "hacc%d%d" % (t, a)) for a in range(2)] for t in range(PACK)]
 
         def first_product(z, t):
@@ -117,35 +112,34 @@ def tile_picked_treeup_relu_p_kernel(tc, x_words, x_scales, w1, w2_words, w2_sca
                     out=h_acc[t][a][:],
                     lhsT=codes.bitcast(FP8X4),
                     lhsT_scale=scales,
-                    rhs=xg[(z, a)].bitcast(FP8X4),
+                    rhs=xg[z][:, cols].bitcast(FP8X4),
                     rhs_scale=xsg[4 * z : P, cols],
                     start=(z == 0),
                     stop=(z == PASSES - 1),
                 )
 
-        nc.vector.tensor_copy(out=xg0[:], in_=xw[0][:].indirect(offs_sb[:]))
+        nc.vector.tensor_copy(out=xg[0][:], in_=xw[0][:].indirect(offs_sb[:]))
         nc.vector.tensor_copy(out=xsg[:], in_=xs[:].indirect(offs_sb[:]))
         for u in range(2):
             cast_w1(nc.scalar.copy, 0, u, 0, P)
         quant_w1(0, 0, 2)
-        xg1 = keep.tile([P, S], U32, name="xg1", tag="w1bf00", align_bytes=64)
-        nc.vector.tensor_copy(out=xg1[:], in_=xw[1][:].indirect(offs_sb[:]))
-        for a in range(2):
-            xg[(1, a)] = xg1[:, a * BANK : (a + 1) * BANK]
-        for t in range(2):
+        xg.append(sb([P, S], U32, "xg1", "w1bf00"))
+        nc.vector.tensor_copy(out=xg[1][:], in_=xw[1][:].indirect(offs_sb[:]))
+        quant_w1(0, 2, 1)
+        for t in range(PACK - 1):
             first_product(0, t)
-        cast_w1(nc.scalar.copy, 1, 0, 0, HALF)
-        cast_w1(nc.vector.tensor_copy, 1, 0, HALF, HALF)
+        cast_w1(nc.scalar.copy, 1, 0, 0, P // 2)
+        cast_w1(nc.vector.tensor_copy, 1, 0, P // 2, P)
         quant_w1(1, 0, 1)
         quant_w1(1, 1, 1)
-        cast_w1(nc.scalar.copy, 1, 1, 0, HALF)
-        cast_w1(nc.vector.tensor_copy, 1, 1, HALF, HALF)
-        quant_w1(0, 2, 2, "w1bf10")
+        cast_w1(nc.scalar.copy, 1, 1, 0, P // 2)
+        cast_w1(nc.vector.tensor_copy, 1, 1, P // 2, P)
         quant_w1(1, 2, 2)
+        quant_w1(0, 3, 1, "w1bf10")
 
-        h = [keep.tile([P, S], F32, name="h%d" % t, align_bytes=64) for t in range(PACK)]
+        h = [sb([P, S], F32, "h%d" % t) for t in range(PACK)]
         for t in range(PACK):
-            if t >= 2:
+            if t == PACK - 1:
                 first_product(0, t)
             first_product(1, t)
             if t == 0:
@@ -154,80 +148,76 @@ def tile_picked_treeup_relu_p_kernel(tc, x_words, x_scales, w1, w2_words, w2_sca
                 nc.scalar.activation(out=h[t][:, 0:BANK], in_=h_acc[t][0][:], func=RELU)
             nc.scalar.activation(out=h[t][:, BANK:S], in_=h_acc[t][1][:], func=RELU)
 
-        def gather(i, t, taken):
-            j0, n, turned = PIECES[i]
+        def gather(t, j0, j1, share_sb, taken):
             nc.vector.tensor_tensor(
-                out=taken[:, t, :],
-                in0=h[t][:].indirect(par_sb[:, j0 // 16 : (j0 + n) // 16]),
-                in1=share_sb[i][:],
-                op=MULT,
+                out=taken[:, t, :], in0=h[t][:].indirect(par_sb[:, j0 // ROWS : j1 // ROWS]), in1=share_sb[:], op=MULT
             )
 
-        turned_in = []
-        for i, (j0, n, turned) in enumerate(PIECES):
-            taken = keep.tile([P, PACK, n], F32, name="taken%d" % j0, tag="chain%d" % (i - 1), align_bytes=64)
-            if not turned:
-                own = keep.tile([P, PACK, n], F32, name="own%d" % j0, align_bytes=64)
-                for t in range(PACK):
-                    nc.sync.dma_start(out=own[:, t, :], in_=h[t][:, j0 : j0 + n])
-                for t in range(PACK):
-                    gather(i, t, taken)
-                direct = (own, taken, j0, n)
-                continue
-            groups = [list(range(b0, min(b0 + 2, n // BLK))) for b0 in range(0, n // BLK, 2)]
-            back = [bank(BACK_BANKS[i][g], "back%d_%d" % (i, g)) for g in range(len(groups))]
-            for u in range(2):
-                z_t = [bank(TURN_BANKS[i][u][g], "zt%d_%d_%d" % (i, g, u)) for g in range(len(groups))]
-                for e in range(2):
-                    for g, blocks in enumerate(groups):
-                        for s, b in enumerate(blocks):
-                            nc.tensor.matmul(
-                                out=z_t[g][:, (2 * s + e) * P : (2 * s + e + 1) * P],
-                                lhsT=h[2 * u + e][:, j0 + b * BLK : j0 + (b + 1) * BLK],
-                                rhs=ident[:],
-                                start=(e == 0 and s == 0),
-                                stop=False,
-                                is_transpose=True,
-                            )
-                for e in range(2):
-                    gather(i, 2 * u + e, taken)
-                    for g, blocks in enumerate(groups):
-                        for s, b in enumerate(blocks):
-                            nc.tensor.matmul(
-                                out=z_t[g][:, (2 * s + e) * P : (2 * s + e + 1) * P],
-                                lhsT=taken[:, 2 * u + e, b * BLK : (b + 1) * BLK],
-                                rhs=ident[:],
-                                start=False,
-                                stop=(e == 1 and b == blocks[-1]),
-                                is_transpose=True,
-                            )
-                for g, blocks in enumerate(groups):
-                    width = len(blocks) * 2 * P
-                    name = "zrows%d_%d_%d" % (i, g, u)
-                    z_rows = keep.tile([P, width], BF16, name=name, tag=name, align_bytes=64)
-                    nc.scalar.copy(
-                        out=z_rows[:].rearrange("p (s m e) -> p s m e", m=P, e=2),
-                        in_=z_t[g][:, 0:width].rearrange("p (s e m) -> p s m e", m=P, e=2),
-                    )
-                    words = z_rows[:].bitcast(F32)
-                    for s in range(len(blocks)):
-                        c0 = (2 * s + u) * P
-                        nc.tensor.transpose(back[g][:, c0 : c0 + P], words[:, s * P : (s + 1) * P], ident[:])
-            for g, blocks in enumerate(groups):
-                width = len(blocks) * 2 * P
-                if i > 0 or g == 0:
-                    cols = n if i == 0 else len(blocks) * BLK
-                    jz = j0 + blocks[0] * BLK
-                    z_in = keep.tile([P, cols * PACK], BF16, name="zin%d" % jz, tag="zin%d" % jz, align_bytes=64)
-                    turned_in.append((z_in, jz, cols))
-                c0 = (j0 + blocks[0] * BLK - jz) * PACK
-                nc.scalar.copy(
-                    out=z_in[:, c0 : c0 + 2 * width].bitcast(F32).rearrange("p (s j u) -> p s j u", j=BLK, u=2),
-                    in_=back[g][:, 0:width].rearrange("p (s u j) -> p s j u", j=BLK, u=2),
-                )
+        def turn(z_t, slot, src, b, start=False, stop=False):
+            nc.tensor.matmul(
+                out=z_t[:, slot * P : (slot + 1) * P],
+                lhsT=src[:, b * BLK : (b + 1) * BLK],
+                rhs=ident[:],
+                start=start,
+                stop=stop,
+                is_transpose=True,
+            )
 
-        z_codes = keep.tile([P, S], U32, name="z_codes", tag="zrows1_0_1", align_bytes=64)
-        z_scales = keep.tile([P, S], U8, name="z_scales", align_bytes=64)
+        def round_and_turn_back(z_t, name, back, slots):
+            z_rows = sb([P, BANK], BF16, name)
+            nc.scalar.copy(
+                out=z_rows[:].rearrange("p (s m e) -> p s m e", m=P, e=2),
+                in_=z_t[:].rearrange("p (s e m) -> p s m e", m=P, e=2),
+            )
+            words = z_rows[:].bitcast(F32)
+            for s, slot in enumerate(slots):
+                nc.tensor.transpose(back[:, slot * P : (slot + 1) * P], words[:, s * P : (s + 1) * P], ident[:])
+
+        def lay_out(z_in, back, blocks):
+            nc.scalar.copy(
+                out=z_in.bitcast(F32).rearrange("p (s j u) -> p s j u", j=BLK, u=2),
+                in_=back[:, 0 : 2 * blocks * P].rearrange("p (s u j) -> p s j u", j=BLK, u=2),
+            )
+
+        taken = sb([P, PACK, TURNED], F32, "taken_turned")
+        back = [bank(6 + g, "back%d" % g) for g in range(2)]
+        for u in range(2):
+            z_t = [bank(2 * u + g, "zt%d%d" % (g, u)) for g in range(2)]
+            for e in range(2):
+                for g in range(2):
+                    for s in range(2):
+                        turn(z_t[g], 2 * s + e, h[2 * u + e], 2 * g + s, start=(e == 0 and s == 0))
+            for e in range(2):
+                gather(2 * u + e, 0, TURNED, share_turned, taken)
+                for g in range(2):
+                    for s in range(2):
+                        turn(z_t[g], 2 * s + e, taken[:, 2 * u + e, :], 2 * g + s, stop=(e == 1 and s == 1))
+            for g in range(2):
+                round_and_turn_back(z_t[g], "zrows%d%d" % (g, u), back[g], (u, 2 + u))
+        z_pairs = sb([P, 4 * BLK * PACK], BF16, "z_pairs")
+        for g in range(2):
+            lay_out(z_pairs[:, g * 2 * BLK * PACK : (g + 1) * 2 * BLK * PACK], back[g], 2)
+
+        last = TURNED // BLK - 1
+        z_t = bank(4, "zt_last")
+        for t in range(PACK):
+            turn(z_t, t, h[t], last, start=(t == 0))
+        for t in range(PACK):
+            turn(z_t, t, taken[:, t, :], last, stop=(t == PACK - 1))
+        back_last = bank(5, "back_last")
+        round_and_turn_back(z_t, "zrows_last", back_last, (0, 1))
+        z_last = sb([P, BLK * PACK], BF16, "z_last")
+        lay_out(z_last[:], back_last, 1)
+
+        own = sb([P, PACK, ADDED], F32, "own")
+        for t in range(PACK):
+            nc.sync.dma_start(out=own[:, t, :], in_=h[t][:, TURNED:S])
+        taken_added = sb([P, PACK, ADDED], F32, "taken_added", "share_turned")
+        for t in range(PACK):
+            gather(t, TURNED, S, share_added, taken_added)
+
+        z_codes = sb([P, S], U32, "z_codes", "zrows11")
+        z_scales = sb([P, S], U8, "z_scales")
 
         def finish(z_in, j0, n, b, copy):
             codes = z_codes[:, j0 : j0 + n]
@@ -243,27 +233,26 @@ def tile_picked_treeup_relu_p_kernel(tc, x_words, x_scales, w1, w2_words, w2_sca
                 start=True,
                 stop=True,
             )
-            res = keep.tile([P, n], F32, name="res%d" % j0, align_bytes=64)
+            res = sb([P, n], F32, "res%d" % j0)
             copy(out=res[:], in_=acc[:, 0:n])
             nc.sync.dma_start(out=out[:, j0 : j0 + n], in_=res[:])
 
-        own, taken, j0, n = direct
-        z_in, jt, nt = turned_in[0]
-        finish(z_in[:], jt, nt, 1, nc.scalar.copy)
-        z_direct = keep.tile([P, 2, BLK * PACK], BF16, name="zdirect", tag="zin0", align_bytes=64)
+        finish(z_pairs[:], 0, 4 * BLK, 0, nc.scalar.copy)
+        z_added = sb([P, ADDED // BLK, BLK * PACK], BF16, "z_added", "z_pairs")
 
-        def add_direct(b):
+        def add(b):
             cols = slice(b * BLK, (b + 1) * BLK)
             nc.vector.tensor_tensor(
-                out=z_direct[:, b, :].rearrange("p (c i t) -> p c t i", i=4, t=PACK),
+                out=z_added[:, b, :].rearrange("p (c i t) -> p c t i", i=4, t=PACK),
                 in0=own[:, :, cols].rearrange("p t (c i) -> p c t i", i=4),
-                in1=taken[:, :, cols].rearrange("p t (c i) -> p c t i", i=4),
+                in1=taken_added[:, :, cols].rearrange("p t (c i) -> p c t i", i=4),
                 op=ADD,
             )
 
-        add_direct(0)
-        z_in, jt, nt = turned_in[1]
-        finish(z_in[:], jt, nt, 2, nc.scalar.copy)
-        add_direct(1)
-        finish(z_direct[:, 0, :], j0, BLK, 3, nc.scalar.copy)
-        finish(z_direct[:, 1, :], j0 + BLK, BLK, 4, nc.vector.tensor_copy)
+        add(0)
+        add(1)
+        finish(z_added[:, 0, :], TURNED, BLK, 1, nc.scalar.copy)
+        finish(z_last[:], last * BLK, BLK, 2, nc.scalar.copy)
+        add(2)
+        finish(z_added[:, 1, :], TURNED + BLK, BLK, 3, nc.scalar.copy)
+        finish(z_added[:, 2, :], TURNED + 2 * BLK, BLK, 4, nc.vector.tensor_copy)

@@ -16,6 +16,7 @@ FP8X4 = mybir.dt.float8_e4m3fn_x4
 MULT = mybir.AluOpType.mult
 ADD = mybir.AluOpType.add
 RELU = mybir.ActivationFunctionType.Relu
+COPY = mybir.ActivationFunctionType.Copy
 
 P = 128
 PACK = 4
@@ -23,8 +24,9 @@ PASSES = K // (P * PACK)
 BANK = 512
 BLK = 128
 ROWS = 16
-TURNED = 5 * BLK
+TURNED = 4 * BLK
 ADDED = S - TURNED
+PAIR = 2 * BLK
 
 
 def tile_picked_treeup_relu_p_kernel(tc, x_words, x_scales, w1, w2_words, w2_scales, share, offs, par, out):
@@ -45,7 +47,6 @@ def tile_picked_treeup_relu_p_kernel(tc, x_words, x_scales, w1, w2_words, w2_sca
         xs = sb([P, T], U8, "xs")
         w1_raw = [sb([P, PACK, H], F32, "w1raw%d" % z) for z in range(PASSES)]
         share_turned = sb([P, TURNED], F32, "share_turned")
-        share_added = sb([P, ADDED], F32, "share_added")
         w2w = sb([P, N], U32, "w2w")
         w2s = sb([P, N], U8, "w2s")
         ident = sb([P, P], F32, "ident")
@@ -73,7 +74,6 @@ def tile_picked_treeup_relu_p_kernel(tc, x_words, x_scales, w1, w2_words, w2_sca
         load_w1(1)
         nc.sync.dma_start(par_sb[:], par)
         nc.sync.dma_start(out=share_turned[:], in_=share[:, 0:TURNED])
-        nc.sync.dma_start(out=share_added[:], in_=share[:, TURNED:S])
         nc.sync.dma_start(out=w2w[:].bitcast(I32), in_=w2_words[0].rearrange("p c r -> p (c r)").bitcast(I32))
         for q in range(4):
             nc.sync.dma_start(
@@ -148,10 +148,24 @@ def tile_picked_treeup_relu_p_kernel(tc, x_words, x_scales, w1, w2_words, w2_sca
                 nc.scalar.activation(out=h[t][:, 0:BANK], in_=h_acc[t][0][:], func=RELU)
             nc.scalar.activation(out=h[t][:, BANK:S], in_=h_acc[t][1][:], func=RELU)
 
+        share_added = sb([P, ADDED], F32, "share_added", "xg0")
+        nc.sync.dma_start(out=share_added[:], in_=share[:, TURNED:S])
+
         def gather(t, j0, j1, share_sb, taken):
             nc.vector.tensor_tensor(
-                out=taken[:, t, :], in0=h[t][:].indirect(par_sb[:, j0 // ROWS : j1 // ROWS]), in1=share_sb[:], op=MULT
+                out=taken, in0=h[t][:].indirect(par_sb[:, j0 // ROWS : j1 // ROWS]), in1=share_sb, op=MULT
             )
+
+        fetched = [sb([P, 2, PAIR], F32, "fetched%d" % pair) for pair in range(2)]
+
+        def fetch_added(pair):
+            j0 = TURNED + pair * PAIR
+            for t in range(2):
+                nc.scalar.activation(
+                    out=fetched[pair][:, t, :],
+                    in_=h[t][:].indirect(par_sb[:, j0 // ROWS : (j0 + PAIR) // ROWS]),
+                    func=COPY,
+                )
 
         def turn(z_t, slot, src, b, start=False, stop=False):
             nc.tensor.matmul(
@@ -163,12 +177,15 @@ def tile_picked_treeup_relu_p_kernel(tc, x_words, x_scales, w1, w2_words, w2_sca
                 is_transpose=True,
             )
 
-        def round_and_turn_back(z_t, name, back, slots):
+        def round_rows(z_t, name):
             z_rows = sb([P, BANK], BF16, name)
             nc.scalar.copy(
                 out=z_rows[:].rearrange("p (s m e) -> p s m e", m=P, e=2),
                 in_=z_t[:].rearrange("p (s e m) -> p s m e", m=P, e=2),
             )
+            return z_rows
+
+        def turn_back(z_rows, back, slots):
             words = z_rows[:].bitcast(F32)
             for s, slot in enumerate(slots):
                 nc.tensor.transpose(back[:, slot * P : (slot + 1) * P], words[:, s * P : (s + 1) * P], ident[:])
@@ -181,6 +198,7 @@ def tile_picked_treeup_relu_p_kernel(tc, x_words, x_scales, w1, w2_words, w2_sca
 
         taken = sb([P, PACK, TURNED], F32, "taken_turned")
         back = [bank(6 + g, "back%d" % g) for g in range(2)]
+        rows = []
         for u in range(2):
             z_t = [bank(2 * u + g, "zt%d%d" % (g, u)) for g in range(2)]
             for e in range(2):
@@ -188,48 +206,60 @@ def tile_picked_treeup_relu_p_kernel(tc, x_words, x_scales, w1, w2_words, w2_sca
                     for s in range(2):
                         turn(z_t[g], 2 * s + e, h[2 * u + e], 2 * g + s, start=(e == 0 and s == 0))
             for e in range(2):
-                gather(2 * u + e, 0, TURNED, share_turned, taken)
+                gather(2 * u + e, 0, TURNED, share_turned[:], taken[:, 2 * u + e, :])
                 for g in range(2):
                     for s in range(2):
                         turn(z_t[g], 2 * s + e, taken[:, 2 * u + e, :], 2 * g + s, stop=(e == 1 and s == 1))
-            for g in range(2):
-                round_and_turn_back(z_t[g], "zrows%d%d" % (g, u), back[g], (u, 2 + u))
-        z_pairs = sb([P, 4 * BLK * PACK], BF16, "z_pairs")
+            fetch_added(u)
+            if u == 1:
+                for g in range(2):
+                    turn_back(rows[g], back[g], (0, 2))
+            rows = [round_rows(z_t[g], "zrows%d%d" % (g, u)) for g in range(2)]
         for g in range(2):
-            lay_out(z_pairs[:, g * 2 * BLK * PACK : (g + 1) * 2 * BLK * PACK], back[g], 2)
-
-        last = TURNED // BLK - 1
-        z_t = bank(4, "zt_last")
-        for t in range(PACK):
-            turn(z_t, t, h[t], last, start=(t == 0))
-        for t in range(PACK):
-            turn(z_t, t, taken[:, t, :], last, stop=(t == PACK - 1))
-        back_last = bank(5, "back_last")
-        round_and_turn_back(z_t, "zrows_last", back_last, (0, 1))
-        z_last = sb([P, BLK * PACK], BF16, "z_last")
-        lay_out(z_last[:], back_last, 1)
+            turn_back(rows[g], back[g], (1, 3))
+        z_turned = sb([P, TURNED * PACK], BF16, "z_turned")
+        for g in range(2):
+            lay_out(z_turned[:, g * PAIR * PACK : (g + 1) * PAIR * PACK], back[g], 2)
 
         own = sb([P, PACK, ADDED], F32, "own")
         for t in range(PACK):
             nc.sync.dma_start(out=own[:, t, :], in_=h[t][:, TURNED:S])
-        taken_added = sb([P, PACK, ADDED], F32, "taken_added", "share_turned")
-        for t in range(PACK):
-            gather(t, TURNED, S, share_added, taken_added)
+        taken_added = [sb([P, PACK, PAIR], F32, "taken_added%d" % pair) for pair in range(2)]
 
-        z_codes = sb([P, S], U32, "z_codes", "zrows11")
-        z_scales = sb([P, S], U8, "z_scales")
+        def gather_added(t, pair):
+            cols = slice(pair * PAIR, (pair + 1) * PAIR)
+            gather(t, TURNED + cols.start, TURNED + cols.stop, share_added[:, cols], taken_added[pair][:, t, :])
+
+        def weigh_fetched(pair):
+            cols = slice(pair * PAIR, (pair + 1) * PAIR)
+            nc.vector.tensor_tensor(
+                out=taken_added[pair][:, 0:2, :],
+                in0=fetched[pair][:],
+                in1=share_added[:, cols].unsqueeze(1).to_broadcast([P, 2, PAIR]),
+                op=MULT,
+            )
+
+        def add(z_in, j0, n):
+            cols = slice(j0, j0 + n)
+            taken_cols = taken_added[j0 // PAIR][:, :, j0 % PAIR : j0 % PAIR + n]
+            nc.vector.tensor_tensor(
+                out=z_in.rearrange("p (c i t) -> p c t i", i=4, t=PACK),
+                in0=own[:, :, cols].rearrange("p t (c i) -> p c t i", i=4),
+                in1=taken_cols.rearrange("p t (c i) -> p c t i", i=4),
+                op=ADD,
+            )
 
         def finish(z_in, j0, n, b, copy):
-            codes = z_codes[:, j0 : j0 + n]
-            scales = z_scales[:, j0 : j0 + n]
-            nc.vector.quantize_mx(out=codes.bitcast(FP8X4), scales=scales, in_=z_in)
+            codes = sb([P, n], U32, "zc%d" % j0)
+            scales = sb([P, n], U8, "zs%d" % j0)
+            nc.vector.quantize_mx(out=codes[:].bitcast(FP8X4), scales=scales[:], in_=z_in)
             acc = bank(b, "oacc%d" % j0)
             nc.tensor.matmul_mx(
                 out=acc[:, 0:n],
                 lhsT=w2w[:].bitcast(FP8X4),
                 lhsT_scale=w2s[:],
-                rhs=codes.bitcast(FP8X4),
-                rhs_scale=scales,
+                rhs=codes[:].bitcast(FP8X4),
+                rhs_scale=scales[:],
                 start=True,
                 stop=True,
             )
@@ -237,22 +267,18 @@ def tile_picked_treeup_relu_p_kernel(tc, x_words, x_scales, w1, w2_words, w2_sca
             copy(out=res[:], in_=acc[:, 0:n])
             nc.sync.dma_start(out=out[:, j0 : j0 + n], in_=res[:])
 
-        finish(z_pairs[:], 0, 4 * BLK, 0, nc.scalar.copy)
-        z_added = sb([P, ADDED // BLK, BLK * PACK], BF16, "z_added", "z_pairs")
-
-        def add(b):
-            cols = slice(b * BLK, (b + 1) * BLK)
-            nc.vector.tensor_tensor(
-                out=z_added[:, b, :].rearrange("p (c i t) -> p c t i", i=4, t=PACK),
-                in0=own[:, :, cols].rearrange("p t (c i) -> p c t i", i=4),
-                in1=taken_added[:, :, cols].rearrange("p t (c i) -> p c t i", i=4),
-                op=ADD,
-            )
-
-        add(0)
-        add(1)
-        finish(z_added[:, 0, :], TURNED, BLK, 1, nc.scalar.copy)
-        finish(z_last[:], last * BLK, BLK, 2, nc.scalar.copy)
-        add(2)
-        finish(z_added[:, 1, :], TURNED + BLK, BLK, 3, nc.scalar.copy)
-        finish(z_added[:, 2, :], TURNED + 2 * BLK, BLK, 4, nc.vector.tensor_copy)
+        z_first = sb([P, PAIR * PACK], BF16, "z_first")
+        gather_added(2, 0)
+        gather_added(3, 0)
+        weigh_fetched(0)
+        gather_added(2, 1)
+        add(z_first[:], 0, PAIR)
+        gather_added(3, 1)
+        weigh_fetched(1)
+        finish(z_first[:], TURNED, PAIR, 7, nc.scalar.copy)
+        finish(z_turned[:], 0, TURNED, 0, nc.scalar.copy)
+        z_second = sb([P, 2, BLK * PACK], BF16, "z_second", "zc%d" % TURNED)
+        for b in range(2):
+            add(z_second[:, b, :], PAIR + b * BLK, BLK)
+        finish(z_second[:, 0, :], TURNED + PAIR, BLK, 1, nc.scalar.copy)
+        finish(z_second[:, 1, :], TURNED + PAIR + BLK, BLK, 2, nc.vector.tensor_copy)

@@ -27,6 +27,7 @@ ROWS = 16
 TURNED = 4 * BLK
 ADDED = S - TURNED
 PAIR = 2 * BLK
+FETCHED = 3
 
 
 def tile_picked_treeup_relu_p_kernel(tc, x_words, x_scales, w1, w2_words, w2_scales, share, offs, par, out):
@@ -156,11 +157,11 @@ def tile_picked_treeup_relu_p_kernel(tc, x_words, x_scales, w1, w2_words, w2_sca
                 out=taken, in0=h[t][:].indirect(par_sb[:, j0 // ROWS : j1 // ROWS]), in1=share_sb, op=MULT
             )
 
-        fetched = [sb([P, 2, PAIR], F32, "fetched%d" % pair) for pair in range(2)]
+        fetched = [sb([P, FETCHED, PAIR], F32, "fetched%d" % pair) for pair in range(2)]
 
         def fetch_added(pair):
             j0 = TURNED + pair * PAIR
-            for t in range(2):
+            for t in range(FETCHED):
                 nc.scalar.activation(
                     out=fetched[pair][:, t, :],
                     in_=h[t][:].indirect(par_sb[:, j0 // ROWS : (j0 + PAIR) // ROWS]),
@@ -196,6 +197,9 @@ def tile_picked_treeup_relu_p_kernel(tc, x_words, x_scales, w1, w2_words, w2_sca
                 in_=back[:, 0 : 2 * blocks * P].rearrange("p (s u j) -> p s j u", j=BLK, u=2),
             )
 
+        for pair in range(2):
+            fetch_added(pair)
+
         taken = sb([P, PACK, TURNED], F32, "taken_turned")
         back = [bank(6 + g, "back%d" % g) for g in range(2)]
         rows = []
@@ -210,7 +214,6 @@ def tile_picked_treeup_relu_p_kernel(tc, x_words, x_scales, w1, w2_words, w2_sca
                 for g in range(2):
                     for s in range(2):
                         turn(z_t[g], 2 * s + e, taken[:, 2 * u + e, :], 2 * g + s, stop=(e == 1 and s == 1))
-            fetch_added(u)
             if u == 1:
                 for g in range(2):
                     turn_back(rows[g], back[g], (0, 2))
@@ -233,9 +236,9 @@ def tile_picked_treeup_relu_p_kernel(tc, x_words, x_scales, w1, w2_words, w2_sca
         def weigh_fetched(pair):
             cols = slice(pair * PAIR, (pair + 1) * PAIR)
             nc.vector.tensor_tensor(
-                out=taken_added[pair][:, 0:2, :],
+                out=taken_added[pair][:, 0:FETCHED, :],
                 in0=fetched[pair][:],
-                in1=share_added[:, cols].unsqueeze(1).to_broadcast([P, 2, PAIR]),
+                in1=share_added[:, cols].unsqueeze(1).to_broadcast([P, FETCHED, PAIR]),
                 op=MULT,
             )
 
@@ -267,18 +270,13 @@ def tile_picked_treeup_relu_p_kernel(tc, x_words, x_scales, w1, w2_words, w2_sca
             copy(out=res[:], in_=acc[:, 0:n])
             nc.sync.dma_start(out=out[:, j0 : j0 + n], in_=res[:])
 
-        z_first = sb([P, PAIR * PACK], BF16, "z_first")
-        gather_added(2, 0)
-        gather_added(3, 0)
-        weigh_fetched(0)
-        gather_added(2, 1)
-        add(z_first[:], 0, PAIR)
-        gather_added(3, 1)
-        weigh_fetched(1)
-        finish(z_first[:], TURNED, PAIR, 7, nc.scalar.copy)
-        finish(z_turned[:], 0, TURNED, 0, nc.scalar.copy)
-        z_second = sb([P, 2, BLK * PACK], BF16, "z_second", "zc%d" % TURNED)
-        for b in range(2):
-            add(z_second[:, b, :], PAIR + b * BLK, BLK)
-        finish(z_second[:, 0, :], TURNED + PAIR, BLK, 1, nc.scalar.copy)
-        finish(z_second[:, 1, :], TURNED + PAIR + BLK, BLK, 2, nc.vector.tensor_copy)
+        z_added = [sb([P, PAIR * PACK], BF16, "z_added%d" % pair) for pair in range(2)]
+        for pair in range(2):
+            gather_added(FETCHED, pair)
+            weigh_fetched(pair)
+        for pair in range(2):
+            add(z_added[pair][:], pair * PAIR, PAIR)
+        for pair in range(2):
+            finish(z_added[pair][:], TURNED + pair * PAIR, PAIR, 6 + pair, nc.scalar.copy)
+        finish(z_turned[:, 0 : PAIR * PACK], 0, PAIR, 0, nc.scalar.copy)
+        finish(z_turned[:, PAIR * PACK : TURNED * PACK], PAIR, PAIR, 1, nc.vector.tensor_copy)

@@ -24,10 +24,10 @@ PASSES = K // (P * PACK)
 BANK = 512
 BLK = 128
 ROWS = 16
-TURNED = 4 * BLK
+TURNED = 5 * BLK
 ADDED = S - TURNED
 PAIR = 2 * BLK
-FETCHED = 3
+FETCHED = 2
 
 
 def tile_picked_treeup_relu_p_kernel(tc, x_words, x_scales, w1, w2_words, w2_scales, share, offs, par, out):
@@ -157,16 +157,11 @@ def tile_picked_treeup_relu_p_kernel(tc, x_words, x_scales, w1, w2_words, w2_sca
                 out=taken, in0=h[t][:].indirect(par_sb[:, j0 // ROWS : j1 // ROWS]), in1=share_sb, op=MULT
             )
 
-        fetched = [sb([P, FETCHED, PAIR], F32, "fetched%d" % pair) for pair in range(2)]
-
-        def fetch_added(pair):
-            j0 = TURNED + pair * PAIR
-            for t in range(FETCHED):
-                nc.scalar.activation(
-                    out=fetched[pair][:, t, :],
-                    in_=h[t][:].indirect(par_sb[:, j0 // ROWS : (j0 + PAIR) // ROWS]),
-                    func=COPY,
-                )
+        fetched = sb([P, FETCHED, ADDED], F32, "fetched")
+        for t in range(FETCHED):
+            nc.scalar.activation(
+                out=fetched[:, t, :], in_=h[t][:].indirect(par_sb[:, TURNED // ROWS : S // ROWS]), func=COPY
+            )
 
         def turn(z_t, slot, src, b, start=False, stop=False):
             nc.tensor.matmul(
@@ -197,11 +192,10 @@ def tile_picked_treeup_relu_p_kernel(tc, x_words, x_scales, w1, w2_words, w2_sca
                 in_=back[:, 0 : 2 * blocks * P].rearrange("p (s u j) -> p s j u", j=BLK, u=2),
             )
 
-        for pair in range(2):
-            fetch_added(pair)
-
         taken = sb([P, PACK, TURNED], F32, "taken_turned")
         back = [bank(6 + g, "back%d" % g) for g in range(2)]
+        last = TURNED // BLK - 1
+        zt_last = bank(4, "zt_last")
         rows = []
         for u in range(2):
             z_t = [bank(2 * u + g, "zt%d%d" % (g, u)) for g in range(2)]
@@ -215,50 +209,53 @@ def tile_picked_treeup_relu_p_kernel(tc, x_words, x_scales, w1, w2_words, w2_sca
                     for s in range(2):
                         turn(z_t[g], 2 * s + e, taken[:, 2 * u + e, :], 2 * g + s, stop=(e == 1 and s == 1))
             if u == 1:
+                for t in range(PACK):
+                    turn(zt_last, t, h[t], last, start=(t == 0))
+                for t in range(PACK):
+                    turn(zt_last, t, taken[:, t, :], last, stop=(t == PACK - 1))
                 for g in range(2):
                     turn_back(rows[g], back[g], (0, 2))
             rows = [round_rows(z_t[g], "zrows%d%d" % (g, u)) for g in range(2)]
         for g in range(2):
             turn_back(rows[g], back[g], (1, 3))
-        z_turned = sb([P, TURNED * PACK], BF16, "z_turned")
+
+        back_last = bank(5, "back_last")
+        turn_back(round_rows(zt_last, "zrows_last"), back_last, (0, 1))
+        z_pairs = sb([P, 2 * PAIR * PACK], BF16, "z_pairs")
         for g in range(2):
-            lay_out(z_turned[:, g * PAIR * PACK : (g + 1) * PAIR * PACK], back[g], 2)
+            lay_out(z_pairs[:, g * PAIR * PACK : (g + 1) * PAIR * PACK], back[g], 2)
+        z_last = sb([P, BLK * PACK], BF16, "z_last")
+        lay_out(z_last[:], back_last, 1)
 
         own = sb([P, PACK, ADDED], F32, "own")
         for t in range(PACK):
             nc.sync.dma_start(out=own[:, t, :], in_=h[t][:, TURNED:S])
-        taken_added = [sb([P, PACK, PAIR], F32, "taken_added%d" % pair) for pair in range(2)]
-
-        def gather_added(t, pair):
-            cols = slice(pair * PAIR, (pair + 1) * PAIR)
-            gather(t, TURNED + cols.start, TURNED + cols.stop, share_added[:, cols], taken_added[pair][:, t, :])
-
-        def weigh_fetched(pair):
-            cols = slice(pair * PAIR, (pair + 1) * PAIR)
-            nc.vector.tensor_tensor(
-                out=taken_added[pair][:, 0:FETCHED, :],
-                in0=fetched[pair][:],
-                in1=share_added[:, cols].unsqueeze(1).to_broadcast([P, FETCHED, PAIR]),
-                op=MULT,
-            )
+        taken_added = sb([P, PACK, ADDED], F32, "taken_added")
+        for t in range(FETCHED, PACK):
+            gather(t, TURNED, S, share_added[:], taken_added[:, t, :])
+            if t == FETCHED:
+                nc.vector.tensor_tensor(
+                    out=taken_added[:, 0:FETCHED, :],
+                    in0=fetched[:],
+                    in1=share_added[:].unsqueeze(1).to_broadcast([P, FETCHED, ADDED]),
+                    op=MULT,
+                )
 
         def add(z_in, j0, n):
             cols = slice(j0, j0 + n)
-            taken_cols = taken_added[j0 // PAIR][:, :, j0 % PAIR : j0 % PAIR + n]
             nc.vector.tensor_tensor(
                 out=z_in.rearrange("p (c i t) -> p c t i", i=4, t=PACK),
                 in0=own[:, :, cols].rearrange("p t (c i) -> p c t i", i=4),
-                in1=taken_cols.rearrange("p t (c i) -> p c t i", i=4),
+                in1=taken_added[:, :, cols].rearrange("p t (c i) -> p c t i", i=4),
                 op=ADD,
             )
 
-        def finish(z_in, j0, n, b, copy):
+        def product(z_in, j0, n, acc):
             codes = sb([P, n], U32, "zc%d" % j0)
             scales = sb([P, n], U8, "zs%d" % j0)
             nc.vector.quantize_mx(out=codes[:].bitcast(FP8X4), scales=scales[:], in_=z_in)
-            acc = bank(b, "oacc%d" % j0)
             nc.tensor.matmul_mx(
-                out=acc[:, 0:n],
+                out=acc,
                 lhsT=w2w[:].bitcast(FP8X4),
                 lhsT_scale=w2s[:],
                 rhs=codes[:].bitcast(FP8X4),
@@ -266,17 +263,30 @@ def tile_picked_treeup_relu_p_kernel(tc, x_words, x_scales, w1, w2_words, w2_sca
                 start=True,
                 stop=True,
             )
+
+        def store(acc, j0, n, copy):
             res = sb([P, n], F32, "res%d" % j0)
-            copy(out=res[:], in_=acc[:, 0:n])
+            copy(out=res[:], in_=acc)
             nc.sync.dma_start(out=out[:, j0 : j0 + n], in_=res[:])
 
-        z_added = [sb([P, PAIR * PACK], BF16, "z_added%d" % pair) for pair in range(2)]
-        for pair in range(2):
-            gather_added(FETCHED, pair)
-            weigh_fetched(pair)
-        for pair in range(2):
-            add(z_added[pair][:], pair * PAIR, PAIR)
-        for pair in range(2):
-            finish(z_added[pair][:], TURNED + pair * PAIR, PAIR, 6 + pair, nc.scalar.copy)
-        finish(z_turned[:, 0 : PAIR * PACK], 0, PAIR, 0, nc.scalar.copy)
-        finish(z_turned[:, PAIR * PACK : TURNED * PACK], PAIR, PAIR, 1, nc.vector.tensor_copy)
+        def finish(z_in, j0, n, b, copy):
+            acc = bank(b, "oacc%d" % j0)
+            product(z_in, j0, n, acc[:, 0:n])
+            store(acc[:, 0:n], j0, n, copy)
+
+        blocks = range(ADDED // BLK)
+        z_added = [sb([P, BLK * PACK], BF16, "z_added%d" % b) for b in blocks]
+        acc = bank(6, "oacc_added")
+        add(z_added[0][:], 0, BLK)
+        for b in blocks:
+            if b + 1 in blocks:
+                add(z_added[b + 1][:], (b + 1) * BLK, BLK)
+            product(z_added[b][:], TURNED + b * BLK, BLK, acc[:, b * BLK : (b + 1) * BLK])
+        store(acc[:, 0:ADDED], TURNED, ADDED, nc.scalar.copy)
+        finish(z_pairs[:, 0 : PAIR * PACK], 0, PAIR, 0, nc.scalar.copy)
+        last_two = [(z_pairs[:, PAIR * PACK : 2 * PAIR * PACK], PAIR, PAIR), (z_last[:], last * BLK, BLK)]
+        accs = [bank(1 + i, "oacc_end%d" % i) for i in range(2)]
+        for acc, (z_in, j0, n) in zip(accs, last_two):
+            product(z_in, j0, n, acc[:, 0:n])
+        for acc, (z_in, j0, n), copy in zip(accs, last_two, (nc.vector.tensor_copy, nc.scalar.copy)):
+            store(acc[:, 0:n], j0, n, copy)

@@ -34,10 +34,14 @@ def tile_picked_treeup_relu_p_kernel(tc, x_words, x_scales, w1, w2_words, w2_sca
     nc = tc.nc
     with ExitStack() as ctx:
         keep = ctx.enter_context(tc.tile_pool(name="keep", bufs=1))
+        late = ctx.enter_context(tc.tile_pool(name="late", bufs=1))
         psum = ctx.enter_context(tc.psum_pool(name="psum", bufs=1))
 
         def sb(shape, dtype, name, reuses=None):
             return keep.tile(shape, dtype, name=name, tag=reuses or name, align_bytes=64)
+
+        def placed(shape, dtype, name, offset):
+            return late.tile(shape, dtype, name=name, offset=offset, align_bytes=64)
 
         def bank(b, name):
             return psum.tile([P, BANK], F32, name=name, tag="bank%d" % b)
@@ -131,10 +135,10 @@ def tile_picked_treeup_relu_p_kernel(tc, x_words, x_scales, w1, w2_words, w2_sca
             first_product(0, t)
         cast_w1(nc.scalar.copy, 1, 0, 0, P // 2)
         cast_w1(nc.vector.tensor_copy, 1, 0, P // 2, P)
-        quant_w1(1, 0, 1)
-        quant_w1(1, 1, 1)
         cast_w1(nc.scalar.copy, 1, 1, 0, P // 2)
         cast_w1(nc.vector.tensor_copy, 1, 1, P // 2, P)
+        quant_w1(1, 0, 1)
+        quant_w1(1, 1, 1)
         quant_w1(1, 2, 2)
         quant_w1(0, 3, 1, "w1bf10")
 
@@ -221,7 +225,7 @@ def tile_picked_treeup_relu_p_kernel(tc, x_words, x_scales, w1, w2_words, w2_sca
 
         back_last = bank(5, "back_last")
         turn_back(round_rows(zt_last, "zrows_last"), back_last, (0, 1))
-        z_pairs = sb([P, 2 * PAIR * PACK], BF16, "z_pairs")
+        z_pairs = placed([P, 2 * PAIR * PACK], BF16, "z_pairs", 0)
         for g in range(2):
             lay_out(z_pairs[:, g * PAIR * PACK : (g + 1) * PAIR * PACK], back[g], 2)
         z_last = sb([P, BLK * PACK], BF16, "z_last")
@@ -231,15 +235,19 @@ def tile_picked_treeup_relu_p_kernel(tc, x_words, x_scales, w1, w2_words, w2_sca
         for t in range(PACK):
             nc.sync.dma_start(out=own[:, t, :], in_=h[t][:, TURNED:S])
         taken_added = sb([P, PACK, ADDED], F32, "taken_added")
-        for t in range(FETCHED, PACK):
-            gather(t, TURNED, S, share_added[:], taken_added[:, t, :])
-            if t == FETCHED:
-                nc.vector.tensor_tensor(
-                    out=taken_added[:, 0:FETCHED, :],
-                    in0=fetched[:],
-                    in1=share_added[:].unsqueeze(1).to_broadcast([P, FETCHED, ADDED]),
-                    op=MULT,
-                )
+
+        def weigh(j0, n):
+            nc.vector.tensor_tensor(
+                out=taken_added[:, 0:FETCHED, j0 : j0 + n],
+                in0=fetched[:, :, j0 : j0 + n],
+                in1=share_added[:, j0 : j0 + n].unsqueeze(1).to_broadcast([P, FETCHED, n]),
+                op=MULT,
+            )
+
+        gather(2, TURNED, S, share_added[:], taken_added[:, 2, :])
+        weigh(0, PAIR)
+        gather(3, TURNED, S, share_added[:], taken_added[:, 3, :])
+        weigh(PAIR, BLK)
 
         def add(z_in, j0, n):
             cols = slice(j0, j0 + n)
@@ -250,8 +258,7 @@ def tile_picked_treeup_relu_p_kernel(tc, x_words, x_scales, w1, w2_words, w2_sca
                 op=ADD,
             )
 
-        def product(z_in, j0, n, acc):
-            codes = sb([P, n], U32, "zc%d" % j0)
+        def product(z_in, j0, n, acc, codes):
             scales = sb([P, n], U8, "zs%d" % j0)
             nc.vector.quantize_mx(out=codes[:].bitcast(FP8X4), scales=scales[:], in_=z_in)
             nc.tensor.matmul_mx(
@@ -269,24 +276,19 @@ def tile_picked_treeup_relu_p_kernel(tc, x_words, x_scales, w1, w2_words, w2_sca
             copy(out=res[:], in_=acc)
             nc.sync.dma_start(out=out[:, j0 : j0 + n], in_=res[:])
 
-        def finish(z_in, j0, n, b, copy):
+        def finish(z_in, j0, n, b, copy, codes=None):
             acc = bank(b, "oacc%d" % j0)
-            product(z_in, j0, n, acc[:, 0:n])
+            product(z_in, j0, n, acc[:, 0:n], sb([P, n], U32, "zc%d" % j0) if codes is None else codes)
             store(acc[:, 0:n], j0, n, copy)
 
-        blocks = range(ADDED // BLK)
-        z_added = [sb([P, BLK * PACK], BF16, "z_added%d" % b) for b in blocks]
-        acc = bank(6, "oacc_added")
-        add(z_added[0][:], 0, BLK)
-        for b in blocks:
-            if b + 1 in blocks:
-                add(z_added[b + 1][:], (b + 1) * BLK, BLK)
-            product(z_added[b][:], TURNED + b * BLK, BLK, acc[:, b * BLK : (b + 1) * BLK])
-        store(acc[:, 0:ADDED], TURNED, ADDED, nc.scalar.copy)
-        finish(z_pairs[:, 0 : PAIR * PACK], 0, PAIR, 0, nc.scalar.copy)
-        last_two = [(z_pairs[:, PAIR * PACK : 2 * PAIR * PACK], PAIR, PAIR), (z_last[:], last * BLK, BLK)]
-        accs = [bank(1 + i, "oacc_end%d" % i) for i in range(2)]
-        for acc, (z_in, j0, n) in zip(accs, last_two):
-            product(z_in, j0, n, acc[:, 0:n])
-        for acc, (z_in, j0, n), copy in zip(accs, last_two, (nc.vector.tensor_copy, nc.scalar.copy)):
-            store(acc[:, 0:n], j0, n, copy)
+        z_added = [sb([P, BLK * PACK], BF16, "z_added%d" % b) for b in range(2)]
+        for b in range(2):
+            add(z_added[b][:], b * BLK, BLK)
+        finish(z_added[0][:], TURNED, BLK, 6, nc.scalar.copy)
+        for g in range(2):
+            finish(z_pairs[:, g * PAIR * PACK : (g + 1) * PAIR * PACK], g * PAIR, PAIR, g, nc.scalar.copy)
+        finish(z_last[:], last * BLK, BLK, 2, nc.scalar.copy)
+        z_end = placed([P, BLK * PACK], BF16, "z_end", 0)
+        add(z_end[:], PAIR, BLK)
+        finish(z_added[1][:], TURNED + BLK, BLK, 3, nc.scalar.copy, placed([P, BLK], U32, "zc_late", 2 * BLK * PACK))
+        finish(z_end[:], TURNED + PAIR, BLK, 4, nc.vector.tensor_copy)

@@ -67,13 +67,19 @@ def tile_picked_treeup_relu_p_kernel(tc, x_words, x_scales, w1, w2_words, w2_sca
             rows = w1[z * P * PACK : (z + 1) * P * PACK, :]
             nc.sync.dma_start(out=w1_raw[z][:], in_=rows.rearrange("(p j) c -> p j c", j=PACK))
 
-        load_x(0)
         nc.sync.dma_start(offs_sb[:], offs)
-        for q in range(4):
+        load_x(0)
+        for q in range(2):
             nc.sync.dma_start(
                 out=xs[32 * q : 32 * q + 4 * PASSES, :].bitcast(I32),
                 in_=x_scales[:, 4 * q : 4 * q + 4, :].bitcast(I32),
             )
+        for q in range(2, 4):
+            for z in range(PASSES):
+                nc.sync.dma_start(
+                    out=xs[32 * q + 4 * z : 32 * q + 4 * z + 4, :].bitcast(I32),
+                    in_=x_scales[z, 4 * q : 4 * q + 4, :].bitcast(I32),
+                )
         load_w1(0)
         load_x(1)
         load_w1(1)
@@ -161,10 +167,12 @@ def tile_picked_treeup_relu_p_kernel(tc, x_words, x_scales, w1, w2_words, w2_sca
                 out=taken, in0=h[t][:].indirect(par_sb[:, j0 // ROWS : j1 // ROWS]), in1=share_sb, op=MULT
             )
 
-        fetched = sb([P, FETCHED, ADDED], F32, "fetched")
-        for t in range(FETCHED):
+        fetched = sb([P, FETCHED + 1, ADDED], F32, "fetched")
+        for t, j0 in ((0, 0), (1, 0), (2, PAIR)):
             nc.scalar.activation(
-                out=fetched[:, t, :], in_=h[t][:].indirect(par_sb[:, TURNED // ROWS : S // ROWS]), func=COPY
+                out=fetched[:, t, j0:ADDED],
+                in_=h[t][:].indirect(par_sb[:, (TURNED + j0) // ROWS : S // ROWS]),
+                func=COPY,
             )
 
         def turn(z_t, slot, src, b, start=False, stop=False):
@@ -236,18 +244,18 @@ def tile_picked_treeup_relu_p_kernel(tc, x_words, x_scales, w1, w2_words, w2_sca
             nc.sync.dma_start(out=own[:, t, :], in_=h[t][:, TURNED:S])
         taken_added = sb([P, PACK, ADDED], F32, "taken_added")
 
-        def weigh(j0, n):
+        def weigh(j0, n, planes):
             nc.vector.tensor_tensor(
-                out=taken_added[:, 0:FETCHED, j0 : j0 + n],
-                in0=fetched[:, :, j0 : j0 + n],
-                in1=share_added[:, j0 : j0 + n].unsqueeze(1).to_broadcast([P, FETCHED, n]),
+                out=taken_added[:, 0:planes, j0 : j0 + n],
+                in0=fetched[:, 0:planes, j0 : j0 + n],
+                in1=share_added[:, j0 : j0 + n].unsqueeze(1).to_broadcast([P, planes, n]),
                 op=MULT,
             )
 
-        gather(2, TURNED, S, share_added[:], taken_added[:, 2, :])
-        weigh(0, PAIR)
+        gather(2, TURNED, TURNED + PAIR, share_added[:, 0:PAIR], taken_added[:, 2, 0:PAIR])
+        weigh(0, PAIR, FETCHED)
         gather(3, TURNED, S, share_added[:], taken_added[:, 3, :])
-        weigh(PAIR, BLK)
+        weigh(PAIR, BLK, FETCHED + 1)
 
         def add(z_in, j0, n):
             cols = slice(j0, j0 + n)

@@ -27,6 +27,7 @@ ROWS = 16
 TURNED = 5 * BLK
 ADDED = S - TURNED
 PAIR = 2 * BLK
+SPLIT = ADDED // 2
 FETCHED = 2
 
 
@@ -136,8 +137,7 @@ def tile_picked_treeup_relu_p_kernel(tc, x_words, x_scales, w1, w2_words, w2_sca
         quant_w1(0, 0, 2)
         xg.append(sb([P, S], U32, "xg1", "w1bf00"))
         nc.vector.tensor_copy(out=xg[1][:], in_=xw[1][:].indirect(offs_sb[:]))
-        quant_w1(0, 2, 1)
-        for t in range(PACK - 1):
+        for t in range(2):
             first_product(0, t)
         cast_w1(nc.scalar.copy, 1, 0, 0, P // 2)
         cast_w1(nc.vector.tensor_copy, 1, 0, P // 2, P)
@@ -146,11 +146,11 @@ def tile_picked_treeup_relu_p_kernel(tc, x_words, x_scales, w1, w2_words, w2_sca
         quant_w1(1, 0, 1)
         quant_w1(1, 1, 1)
         quant_w1(1, 2, 2)
-        quant_w1(0, 3, 1, "w1bf10")
+        quant_w1(0, 2, 2, "w1bf10")
 
         h = [sb([P, S], F32, "h%d" % t) for t in range(PACK)]
         for t in range(PACK):
-            if t == PACK - 1:
+            if t >= 2:
                 first_product(0, t)
             first_product(1, t)
             if t == 0:
@@ -168,7 +168,7 @@ def tile_picked_treeup_relu_p_kernel(tc, x_words, x_scales, w1, w2_words, w2_sca
             )
 
         fetched = sb([P, FETCHED + 1, ADDED], F32, "fetched")
-        for t, j0 in ((0, 0), (1, 0), (2, PAIR)):
+        for t, j0 in ((0, 0), (1, 0), (2, SPLIT)):
             nc.scalar.activation(
                 out=fetched[:, t, j0:ADDED],
                 in_=h[t][:].indirect(par_sb[:, (TURNED + j0) // ROWS : S // ROWS]),
@@ -252,10 +252,10 @@ def tile_picked_treeup_relu_p_kernel(tc, x_words, x_scales, w1, w2_words, w2_sca
                 op=MULT,
             )
 
-        gather(2, TURNED, TURNED + PAIR, share_added[:, 0:PAIR], taken_added[:, 2, 0:PAIR])
-        weigh(0, PAIR, FETCHED)
+        gather(2, TURNED, TURNED + SPLIT, share_added[:, 0:SPLIT], taken_added[:, 2, 0:SPLIT])
+        weigh(0, SPLIT, FETCHED)
         gather(3, TURNED, S, share_added[:], taken_added[:, 3, :])
-        weigh(PAIR, BLK, FETCHED + 1)
+        weigh(SPLIT, ADDED - SPLIT, FETCHED + 1)
 
         def add(z_in, j0, n):
             cols = slice(j0, j0 + n)
@@ -298,5 +298,8 @@ def tile_picked_treeup_relu_p_kernel(tc, x_words, x_scales, w1, w2_words, w2_sca
         finish(z_last[:], last * BLK, BLK, 2, nc.scalar.copy)
         z_end = placed([P, BLK * PACK], BF16, "z_end", 0)
         add(z_end[:], PAIR, BLK)
-        finish(z_added[1][:], TURNED + BLK, BLK, 3, nc.scalar.copy, placed([P, BLK], U32, "zc_late", 2 * BLK * PACK))
-        finish(z_end[:], TURNED + PAIR, BLK, 4, nc.vector.tensor_copy)
+        accs = [bank(3 + b, "oacc_end%d" % b) for b in range(2)]
+        product(z_added[1][:], TURNED + BLK, BLK, accs[0][:, 0:BLK], placed([P, BLK], U32, "zc_late", 2 * BLK * PACK))
+        product(z_end[:], TURNED + PAIR, BLK, accs[1][:, 0:BLK], sb([P, BLK], U32, "zc_end"))
+        for b in range(2):
+            store(accs[b][:, 0:BLK], TURNED + (1 + b) * BLK, BLK, nc.vector.tensor_copy)

@@ -24,11 +24,12 @@ PASSES = K // (P * PACK)
 BANK = 512
 BLK = 128
 ROWS = 16
+PAIR = 2 * BLK
+HALF = P // 2
 TURNED = 5 * BLK
 ADDED = S - TURNED
-PAIR = 2 * BLK
-SPLIT = ADDED // 2
 FETCHED = 2
+SPLIT = PAIR
 
 
 def tile_picked_treeup_relu_p_kernel(tc, x_words, x_scales, w1, w2_words, w2_scales, share, offs, par, out):
@@ -139,10 +140,9 @@ def tile_picked_treeup_relu_p_kernel(tc, x_words, x_scales, w1, w2_words, w2_sca
         nc.vector.tensor_copy(out=xg[1][:], in_=xw[1][:].indirect(offs_sb[:]))
         for t in range(2):
             first_product(0, t)
-        cast_w1(nc.scalar.copy, 1, 0, 0, P // 2)
-        cast_w1(nc.vector.tensor_copy, 1, 0, P // 2, P)
-        cast_w1(nc.scalar.copy, 1, 1, 0, P // 2)
-        cast_w1(nc.vector.tensor_copy, 1, 1, P // 2, P)
+        for u in range(2):
+            cast_w1(nc.scalar.copy, 1, u, 0, HALF)
+            cast_w1(nc.vector.tensor_copy, 1, u, HALF, P)
         quant_w1(1, 0, 1)
         quant_w1(1, 1, 1)
         quant_w1(1, 2, 2)
@@ -162,13 +162,14 @@ def tile_picked_treeup_relu_p_kernel(tc, x_words, x_scales, w1, w2_words, w2_sca
         share_added = sb([P, ADDED], F32, "share_added", "xg0")
         nc.sync.dma_start(out=share_added[:], in_=share[:, TURNED:S])
 
-        def gather(t, j0, j1, share_sb, taken):
+        def gather(t, j0, j1, share_sb, dst):
             nc.vector.tensor_tensor(
-                out=taken, in0=h[t][:].indirect(par_sb[:, j0 // ROWS : j1 // ROWS]), in1=share_sb, op=MULT
+                out=dst, in0=h[t][:].indirect(par_sb[:, j0 // ROWS : j1 // ROWS]), in1=share_sb, op=MULT
             )
 
         fetched = sb([P, FETCHED + 1, ADDED], F32, "fetched")
-        for t, j0 in ((0, 0), (1, 0), (2, SPLIT)):
+        for t in range(FETCHED + 1):
+            j0 = 0 if t < FETCHED else SPLIT
             nc.scalar.activation(
                 out=fetched[:, t, j0:ADDED],
                 in_=h[t][:].indirect(par_sb[:, (TURNED + j0) // ROWS : S // ROWS]),
@@ -252,9 +253,9 @@ def tile_picked_treeup_relu_p_kernel(tc, x_words, x_scales, w1, w2_words, w2_sca
                 op=MULT,
             )
 
-        gather(2, TURNED, TURNED + SPLIT, share_added[:, 0:SPLIT], taken_added[:, 2, 0:SPLIT])
+        gather(FETCHED, TURNED, TURNED + SPLIT, share_added[:, 0:SPLIT], taken_added[:, FETCHED, 0:SPLIT])
         weigh(0, SPLIT, FETCHED)
-        gather(3, TURNED, S, share_added[:], taken_added[:, 3, :])
+        gather(PACK - 1, TURNED, S, share_added[:], taken_added[:, PACK - 1, :])
         weigh(SPLIT, ADDED - SPLIT, FETCHED + 1)
 
         def add(z_in, j0, n):
@@ -284,22 +285,23 @@ def tile_picked_treeup_relu_p_kernel(tc, x_words, x_scales, w1, w2_words, w2_sca
             copy(out=res[:], in_=acc)
             nc.sync.dma_start(out=out[:, j0 : j0 + n], in_=res[:])
 
-        def finish(z_in, j0, n, b, copy, codes=None):
+        def finish(z_in, j0, n, b):
             acc = bank(b, "oacc%d" % j0)
-            product(z_in, j0, n, acc[:, 0:n], sb([P, n], U32, "zc%d" % j0) if codes is None else codes)
-            store(acc[:, 0:n], j0, n, copy)
+            product(z_in, j0, n, acc[:, 0:n], sb([P, n], U32, "zc%d" % j0))
+            store(acc[:, 0:n], j0, n, nc.scalar.copy)
 
         z_added = [sb([P, BLK * PACK], BF16, "z_added%d" % b) for b in range(2)]
         for b in range(2):
             add(z_added[b][:], b * BLK, BLK)
-        finish(z_added[0][:], TURNED, BLK, 6, nc.scalar.copy)
+        finish(z_added[0][:], TURNED, BLK, 6)
         for g in range(2):
-            finish(z_pairs[:, g * PAIR * PACK : (g + 1) * PAIR * PACK], g * PAIR, PAIR, g, nc.scalar.copy)
-        finish(z_last[:], last * BLK, BLK, 2, nc.scalar.copy)
+            finish(z_pairs[:, g * PAIR * PACK : (g + 1) * PAIR * PACK], g * PAIR, PAIR, g)
+        finish(z_last[:], last * BLK, BLK, 2)
         z_end = placed([P, BLK * PACK], BF16, "z_end", 0)
         add(z_end[:], PAIR, BLK)
         accs = [bank(3 + b, "oacc_end%d" % b) for b in range(2)]
-        product(z_added[1][:], TURNED + BLK, BLK, accs[0][:, 0:BLK], placed([P, BLK], U32, "zc_late", 2 * BLK * PACK))
+        behind_z_end = 2 * BLK * PACK
+        product(z_added[1][:], TURNED + BLK, BLK, accs[0][:, 0:BLK], placed([P, BLK], U32, "zc_late", behind_z_end))
         product(z_end[:], TURNED + PAIR, BLK, accs[1][:, 0:BLK], sb([P, BLK], U32, "zc_end"))
         for b in range(2):
             store(accs[b][:, 0:BLK], TURNED + (1 + b) * BLK, BLK, nc.vector.tensor_copy)

@@ -28,8 +28,7 @@ PAIR = 2 * BLK
 HALF = P // 2
 TURNED = 5 * BLK
 ADDED = S - TURNED
-FETCHED = 2
-SPLIT = PAIR
+FETCHED = 3
 
 
 def tile_picked_treeup_relu_p_kernel(tc, x_words, x_scales, w1, w2_words, w2_scales, share, offs, par, out):
@@ -115,18 +114,21 @@ def tile_picked_treeup_relu_p_kernel(tc, x_words, x_scales, w1, w2_words, w2_sca
 
         xsg = sb([P, S], U8, "xsg")
         xg = [sb([P, S], U32, "xg0")]
-        h_acc = [[bank(2 * t + a, "hacc%d%d" % (t, a)) for a in range(2)] for t in range(PACK)]
+        spans = [[(0, 0, PAIR), (1, PAIR, PAIR), (6, 2 * PAIR, PAIR), (7, 3 * PAIR, PAIR)]]
+        spans = spans + [[(2 * t + a, a * BANK, BANK) for a in range(2)] for t in range(1, PACK)]
+        h_acc = {}
 
         def first_product(z, t):
             codes, scales = w1_mx[(z, t)]
-            for a in range(2):
-                cols = slice(a * BANK, (a + 1) * BANK)
+            for b, j0, n in spans[t]:
+                if z == 0:
+                    h_acc[(t, j0)] = bank(b, "hacc%d_%d" % (t, j0))
                 nc.tensor.matmul_mx(
-                    out=h_acc[t][a][:],
+                    out=h_acc[(t, j0)][:, 0:n],
                     lhsT=codes.bitcast(FP8X4),
                     lhsT_scale=scales,
-                    rhs=xg[z][:, cols].bitcast(FP8X4),
-                    rhs_scale=xsg[4 * z : P, cols],
+                    rhs=xg[z][:, j0 : j0 + n].bitcast(FP8X4),
+                    rhs_scale=xsg[4 * z : P, j0 : j0 + n],
                     start=(z == 0),
                     stop=(z == PASSES - 1),
                 )
@@ -153,11 +155,11 @@ def tile_picked_treeup_relu_p_kernel(tc, x_words, x_scales, w1, w2_words, w2_sca
             if t >= 2:
                 first_product(0, t)
             first_product(1, t)
-            if t == 0:
-                nc.vector.tensor_scalar_max(out=h[t][:, 0:BANK], in0=h_acc[t][0][:], scalar1=0.0)
-            else:
-                nc.scalar.activation(out=h[t][:, 0:BANK], in_=h_acc[t][0][:], func=RELU)
-            nc.scalar.activation(out=h[t][:, BANK:S], in_=h_acc[t][1][:], func=RELU)
+            for i, (b, j0, n) in enumerate(spans[t]):
+                if t == 0 and i in (1, 2):
+                    nc.vector.tensor_scalar_max(out=h[t][:, j0 : j0 + n], in0=h_acc[(t, j0)][:, 0:n], scalar1=0.0)
+                else:
+                    nc.scalar.activation(out=h[t][:, j0 : j0 + n], in_=h_acc[(t, j0)][:, 0:n], func=RELU)
 
         share_added = sb([P, ADDED], F32, "share_added", "xg0")
         nc.sync.dma_start(out=share_added[:], in_=share[:, TURNED:S])
@@ -167,13 +169,10 @@ def tile_picked_treeup_relu_p_kernel(tc, x_words, x_scales, w1, w2_words, w2_sca
                 out=dst, in0=h[t][:].indirect(par_sb[:, j0 // ROWS : j1 // ROWS]), in1=share_sb, op=MULT
             )
 
-        fetched = sb([P, FETCHED + 1, ADDED], F32, "fetched")
-        for t in range(FETCHED + 1):
-            j0 = 0 if t < FETCHED else SPLIT
+        fetched = sb([P, FETCHED, ADDED], F32, "fetched")
+        for t in range(FETCHED):
             nc.scalar.activation(
-                out=fetched[:, t, j0:ADDED],
-                in_=h[t][:].indirect(par_sb[:, (TURNED + j0) // ROWS : S // ROWS]),
-                func=COPY,
+                out=fetched[:, t, :], in_=h[t][:].indirect(par_sb[:, TURNED // ROWS : S // ROWS]), func=COPY
             )
 
         def turn(z_t, slot, src, b, start=False, stop=False):
@@ -253,10 +252,9 @@ def tile_picked_treeup_relu_p_kernel(tc, x_words, x_scales, w1, w2_words, w2_sca
                 op=MULT,
             )
 
-        gather(FETCHED, TURNED, TURNED + SPLIT, share_added[:, 0:SPLIT], taken_added[:, FETCHED, 0:SPLIT])
-        weigh(0, SPLIT, FETCHED)
         gather(PACK - 1, TURNED, S, share_added[:], taken_added[:, PACK - 1, :])
-        weigh(SPLIT, ADDED - SPLIT, FETCHED + 1)
+        weigh(0, PAIR, FETCHED)
+        weigh(PAIR, ADDED - PAIR, FETCHED)
 
         def add(z_in, j0, n):
             cols = slice(j0, j0 + n)

@@ -39,10 +39,10 @@ def tile_picked_treeup_relu_p_kernel(tc, x_words, x_scales, w1, w2_words, w2_sca
         psum = ctx.enter_context(tc.psum_pool(name="psum", bufs=1))
 
         def sb(shape, dtype, name, reuses=None):
-            return keep.tile(shape, dtype, name=name, tag=reuses or name, align_bytes=64)
+            return keep.tile(shape, dtype, name=name, tag=reuses or name, align_bytes=256)
 
         def placed(shape, dtype, name, offset):
-            return late.tile(shape, dtype, name=name, offset=offset, align_bytes=64)
+            return late.tile(shape, dtype, name=name, offset=offset, align_bytes=256)
 
         def bank(b, name):
             return psum.tile([P, BANK], F32, name=name, tag="bank%d" % b)

@@ -55,35 +55,39 @@ def tile_picked_treeup_relu_p_kernel(tc, x_words, x_scales, w1, w2_words, w2_sca
         share_turned = sb([P, TURNED], F32, "share_turned")
         w2w = sb([P, N], U32, "w2w")
         w2s = sb([P, N], U8, "w2s")
+        ident_raw = sb([P, P], F32, "ident_raw")
         ident = sb([P, P], F32, "ident")
 
         nc.gpsimd.memset(xs[:].bitcast(I32), 0)
-        nc.vector.memset(w2s[:].bitcast(I32), 0)
-        make_identity(nc, ident[:])
+        nc.gpsimd.memset(ident_raw[:], 0.0)
+        nc.scalar.copy(out=ident[:], in_=ident_raw[:])
+        nc.gpsimd.memset(w2s[:].bitcast(I32), 0)
+        make_identity(nc, ident[:], nomemset=True)
 
         def load_x(z):
             nc.sync.dma_start(out=xw[z][:].bitcast(I32), in_=x_words[z].rearrange("p c r -> p (c r)").bitcast(I32))
 
-        def load_w1(z):
-            rows = w1[z * P * PACK : (z + 1) * P * PACK, :]
-            nc.sync.dma_start(out=w1_raw[z][:], in_=rows.rearrange("(p j) c -> p j c", j=PACK))
+        def load_w1(z, j0, j1):
+            rows = w1[z * P * PACK : (z + 1) * P * PACK, :].rearrange("(p j) c -> p j c", j=PACK)
+            nc.sync.dma_start(out=w1_raw[z][:, j0:j1, :], in_=rows[:, j0:j1, :])
 
         nc.sync.dma_start(offs_sb[:], offs)
-        load_x(0)
-        for q in range(2):
+        load_w1(0, 0, 2)
+        for q in range(3):
             nc.sync.dma_start(
                 out=xs[32 * q : 32 * q + 4 * PASSES, :].bitcast(I32),
                 in_=x_scales[:, 4 * q : 4 * q + 4, :].bitcast(I32),
             )
-        for q in range(2, 4):
+        for q in range(3, 4):
             for z in range(PASSES):
                 nc.sync.dma_start(
                     out=xs[32 * q + 4 * z : 32 * q + 4 * z + 4, :].bitcast(I32),
                     in_=x_scales[z, 4 * q : 4 * q + 4, :].bitcast(I32),
                 )
-        load_w1(0)
+        load_w1(0, 2, PACK)
+        load_x(0)
         load_x(1)
-        load_w1(1)
+        load_w1(1, 0, PACK)
         nc.sync.dma_start(par_sb[:], par)
         nc.sync.dma_start(out=share_turned[:], in_=share[:, 0:TURNED])
         nc.sync.dma_start(out=w2w[:].bitcast(I32), in_=w2_words[0].rearrange("p c r -> p (c r)").bitcast(I32))
@@ -113,9 +117,9 @@ def tile_picked_treeup_relu_p_kernel(tc, x_words, x_scales, w1, w2_words, w2_sca
                 w1_mx[(z, t0 + i)] = (codes[:, i * P : (i + 1) * P], scales[:, i * P : (i + 1) * P])
 
         xsg = sb([P, S], U8, "xsg")
-        xg = [sb([P, S], U32, "xg0")]
-        spans = [[(0, 0, PAIR), (1, PAIR, PAIR), (6, 2 * PAIR, PAIR), (7, 3 * PAIR, PAIR)]]
-        spans = spans + [[(2 * t + a, a * BANK, BANK) for a in range(2)] for t in range(1, PACK)]
+        xg = [sb([P, S], U32, "xg%d" % z) for z in range(PASSES)]
+        spans = [[(4 * (1 - t) + a, a * PAIR, PAIR) for a in range(4)] for t in range(2)]
+        spans = spans + [[(2 * t + a, a * BANK, BANK) for a in range(2)] for t in range(2, PACK)]
         h_acc = {}
 
         def first_product(z, t):
@@ -133,13 +137,14 @@ def tile_picked_treeup_relu_p_kernel(tc, x_words, x_scales, w1, w2_words, w2_sca
                     stop=(z == PASSES - 1),
                 )
 
-        nc.vector.tensor_copy(out=xg[0][:], in_=xw[0][:].indirect(offs_sb[:]))
         nc.vector.tensor_copy(out=xsg[:], in_=xs[:].indirect(offs_sb[:]))
+        cast_w1(nc.scalar.copy, 0, 0, 0, P)
+        cast_w1(nc.scalar.copy, 0, 1, 0, HALF)
+        cast_w1(nc.vector.tensor_copy, 0, 1, HALF, P)
         for u in range(2):
-            cast_w1(nc.scalar.copy, 0, u, 0, P)
-        quant_w1(0, 0, 2)
-        xg.append(sb([P, S], U32, "xg1", "w1bf00"))
-        nc.vector.tensor_copy(out=xg[1][:], in_=xw[1][:].indirect(offs_sb[:]))
+            quant_w1(0, 2 * u, 2)
+        for z in range(PASSES):
+            nc.vector.tensor_copy(out=xg[z][:], in_=xw[z][:].indirect(offs_sb[:]))
         for t in range(2):
             first_product(0, t)
         for u in range(2):
@@ -148,7 +153,6 @@ def tile_picked_treeup_relu_p_kernel(tc, x_words, x_scales, w1, w2_words, w2_sca
         quant_w1(1, 0, 1)
         quant_w1(1, 1, 1)
         quant_w1(1, 2, 2)
-        quant_w1(0, 2, 2, "w1bf10")
 
         h = [sb([P, S], F32, "h%d" % t) for t in range(PACK)]
         for t in range(PACK):
@@ -301,5 +305,5 @@ def tile_picked_treeup_relu_p_kernel(tc, x_words, x_scales, w1, w2_words, w2_sca
         behind_z_end = 2 * BLK * PACK
         product(z_added[1][:], TURNED + BLK, BLK, accs[0][:, 0:BLK], placed([P, BLK], U32, "zc_late", behind_z_end))
         product(z_end[:], TURNED + PAIR, BLK, accs[1][:, 0:BLK], sb([P, BLK], U32, "zc_end"))
-        for b in range(2):
-            store(accs[b][:, 0:BLK], TURNED + (1 + b) * BLK, BLK, nc.vector.tensor_copy)
+        for b, copy in enumerate((nc.scalar.copy, nc.vector.tensor_copy)):
+            store(accs[b][:, 0:BLK], TURNED + (1 + b) * BLK, BLK, copy)

@@ -29,6 +29,8 @@ HALF = P // 2
 TURNED = 5 * BLK
 ADDED = S - TURNED
 FETCHED = 3
+SPREAD = 4
+FREED = 8192
 
 
 def tile_picked_treeup_relu_p_kernel(tc, x_words, x_scales, w1, w2_words, w2_scales, share, offs, par, out):
@@ -49,19 +51,18 @@ def tile_picked_treeup_relu_p_kernel(tc, x_words, x_scales, w1, w2_words, w2_sca
 
         offs_sb = keep.tile([P, S // ROWS], U16, name="offs_sb")
         par_sb = keep.tile([P, S // ROWS], U16, name="par_sb")
-        xw = [sb([P, T], U32, "xw%d" % z) for z in range(PASSES)]
+        xw = [placed([P, T], U32, "xw0", FREED), sb([P, T], U32, "xw1")]
         xs = sb([P, T], U8, "xs")
-        w1_raw = [sb([P, PACK, H], F32, "w1raw%d" % z) for z in range(PASSES)]
-        share_turned = sb([P, TURNED], F32, "share_turned")
-        w2w = sb([P, N], U32, "w2w")
-        w2s = sb([P, N], U8, "w2s")
-        ident_raw = sb([P, P], F32, "ident_raw")
+        xsg = sb([P, S], U8, "xsg")
+        planes = sb([P, PASSES, S], U8, "planes")
+        w1_raw = [sb([P, PACK, H], F32, "w1raw0")]
+        zeros = sb([P, P], F32, "zeros")
         ident = sb([P, P], F32, "ident")
 
         nc.gpsimd.memset(xs[:].bitcast(I32), 0)
-        nc.gpsimd.memset(ident_raw[:], 0.0)
-        nc.scalar.copy(out=ident[:], in_=ident_raw[:])
-        nc.gpsimd.memset(w2s[:].bitcast(I32), 0)
+        nc.gpsimd.memset(zeros[:], 0.0)
+        nc.scalar.copy(out=ident[:], in_=zeros[:])
+        nc.gpsimd.memset(planes[:].rearrange("p z s -> p (z s)").bitcast(I32), 0)
         make_identity(nc, ident[:], nomemset=True)
 
         def load_x(z):
@@ -71,31 +72,28 @@ def tile_picked_treeup_relu_p_kernel(tc, x_words, x_scales, w1, w2_words, w2_sca
             rows = w1[z * P * PACK : (z + 1) * P * PACK, :].rearrange("(p j) c -> p j c", j=PACK)
             nc.sync.dma_start(out=w1_raw[z][:, j0:j1, :], in_=rows[:, j0:j1, :])
 
-        nc.sync.dma_start(offs_sb[:], offs)
-        load_w1(0, 0, 2)
-        for q in range(3):
-            nc.sync.dma_start(
-                out=xs[32 * q : 32 * q + 4 * PASSES, :].bitcast(I32),
-                in_=x_scales[:, 4 * q : 4 * q + 4, :].bitcast(I32),
-            )
-        for q in range(3, 4):
-            for z in range(PASSES):
+        def move_scales(z):
+            for q in (0, 2, 1, 3):
+                first = SPREAD * (16 * z + 4 * q)
                 nc.sync.dma_start(
-                    out=xs[32 * q + 4 * z : 32 * q + 4 * z + 4, :].bitcast(I32),
-                    in_=x_scales[z, 4 * q : 4 * q + 4, :].bitcast(I32),
+                    out=planes[32 * q + 4 * z : 32 * q + 4 * z + 4, z, :].bitcast(I32),
+                    in_=xsg[first : first + 4 * SPREAD : SPREAD, :].bitcast(I32),
                 )
-        load_w1(0, 2, PACK)
+
+        load_w1(0, 0, 1)
+        nc.sync.dma_start(offs_sb[:], offs)
+        nc.sync.dma_start(
+            out=xs[0 : 32 * SPREAD : SPREAD, :].bitcast(I32), in_=x_scales.rearrange("z q c -> (z q) c").bitcast(I32)
+        )
         load_x(0)
+        load_w1(0, 1, PACK)
         load_x(1)
-        load_w1(1, 0, PACK)
         nc.sync.dma_start(par_sb[:], par)
-        nc.sync.dma_start(out=share_turned[:], in_=share[:, 0:TURNED])
-        nc.sync.dma_start(out=w2w[:].bitcast(I32), in_=w2_words[0].rearrange("p c r -> p (c r)").bitcast(I32))
-        for q in range(4):
-            nc.sync.dma_start(
-                out=w2s[32 * q : 32 * q + 4, :].bitcast(I32),
-                in_=w2_scales[0, 4 * q : 4 * q + 4, :].bitcast(I32),
-            )
+        nc.vector.tensor_copy(out=xsg[:], in_=xs[:].indirect(offs_sb[:]))
+        move_scales(0)
+        w1_raw.append(sb([P, PACK, H], F32, "w1raw1", "xs"))
+        load_w1(1, 0, PACK)
+        move_scales(1)
 
         w1_bf = {(z, u): sb([P, 2, P, PACK], BF16, "w1bf%d%d" % (z, u)) for z in range(PASSES) for u in range(2)}
         w1_mx = {}
@@ -116,7 +114,6 @@ def tile_picked_treeup_relu_p_kernel(tc, x_words, x_scales, w1, w2_words, w2_sca
             for i in range(planes):
                 w1_mx[(z, t0 + i)] = (codes[:, i * P : (i + 1) * P], scales[:, i * P : (i + 1) * P])
 
-        xsg = sb([P, S], U8, "xsg")
         xg = [sb([P, S], U32, "xg%d" % z) for z in range(PASSES)]
         spans = [[(4 * (1 - t) + a, a * PAIR, PAIR) for a in range(4)] for t in range(2)]
         spans = spans + [[(2 * t + a, a * BANK, BANK) for a in range(2)] for t in range(2, PACK)]
@@ -132,19 +129,29 @@ def tile_picked_treeup_relu_p_kernel(tc, x_words, x_scales, w1, w2_words, w2_sca
                     lhsT=codes.bitcast(FP8X4),
                     lhsT_scale=scales,
                     rhs=xg[z][:, j0 : j0 + n].bitcast(FP8X4),
-                    rhs_scale=xsg[4 * z : P, j0 : j0 + n],
+                    rhs_scale=planes[4 * z : P, z, j0 : j0 + n],
                     start=(z == 0),
                     stop=(z == PASSES - 1),
                 )
 
-        nc.vector.tensor_copy(out=xsg[:], in_=xs[:].indirect(offs_sb[:]))
+        nc.vector.tensor_copy(out=xg[0][:], in_=xw[0][:].indirect(offs_sb[:]))
         cast_w1(nc.scalar.copy, 0, 0, 0, P)
         cast_w1(nc.scalar.copy, 0, 1, 0, HALF)
         cast_w1(nc.vector.tensor_copy, 0, 1, HALF, P)
         for u in range(2):
             quant_w1(0, 2 * u, 2)
-        for z in range(PASSES):
-            nc.vector.tensor_copy(out=xg[z][:], in_=xw[z][:].indirect(offs_sb[:]))
+        nc.vector.tensor_copy(out=xg[1][:], in_=xw[1][:].indirect(offs_sb[:]))
+        share_turned = placed([P, TURNED], F32, "share_turned", FREED)
+        w2w = placed([P, N], U32, "w2w", FREED + 4 * TURNED)
+        w2s = placed([P, N], U8, "w2s", FREED + 4 * TURNED + 4 * N)
+        nc.sync.dma_start(out=share_turned[:], in_=share[:, 0:TURNED])
+        nc.sync.dma_start(out=w2w[:].bitcast(I32), in_=w2_words[0].rearrange("p c r -> p (c r)").bitcast(I32))
+        nc.gpsimd.memset(w2s[:].bitcast(I32), 0)
+        for q in range(4):
+            nc.sync.dma_start(
+                out=w2s[32 * q : 32 * q + 4, :].bitcast(I32),
+                in_=w2_scales[0, 4 * q : 4 * q + 4, :].bitcast(I32),
+            )
         for t in range(2):
             first_product(0, t)
         for u in range(2):

@@ -136,15 +136,16 @@ def tile_picked_treeup_relu_p_kernel(tc, x_words, x_scales, w1, w2_words, w2_sca
 
         nc.vector.tensor_copy(out=xg[0][:], in_=xw[0][:].indirect(offs_sb[:]))
         cast_w1(nc.scalar.copy, 0, 0, 0, P)
-        cast_w1(nc.scalar.copy, 0, 1, 0, HALF)
-        cast_w1(nc.vector.tensor_copy, 0, 1, HALF, P)
+        cast_w1(nc.scalar.copy, 0, 1, 0, P // 4)
+        cast_w1(nc.vector.tensor_copy, 0, 1, P // 4, P)
         for u in range(2):
             quant_w1(0, 2 * u, 2)
         nc.vector.tensor_copy(out=xg[1][:], in_=xw[1][:].indirect(offs_sb[:]))
-        share_turned = placed([P, TURNED], F32, "share_turned", FREED)
-        w2w = placed([P, N], U32, "w2w", FREED + 4 * TURNED)
-        w2s = placed([P, N], U8, "w2s", FREED + 4 * TURNED + 4 * N)
-        nc.sync.dma_start(out=share_turned[:], in_=share[:, 0:TURNED])
+        share_sb = placed([P, S], F32, "share_sb", FREED)
+        share_turned, share_added = share_sb[:, 0:TURNED], share_sb[:, TURNED:S]
+        w2w = placed([P, N], U32, "w2w", FREED + 4 * S)
+        w2s = placed([P, N], U8, "w2s", FREED + 4 * S + 4 * N)
+        nc.sync.dma_start(out=share_sb[:], in_=share)
         nc.sync.dma_start(out=w2w[:].bitcast(I32), in_=w2_words[0].rearrange("p c r -> p (c r)").bitcast(I32))
         nc.gpsimd.memset(w2s[:].bitcast(I32), 0)
         for q in range(4):
@@ -171,9 +172,6 @@ def tile_picked_treeup_relu_p_kernel(tc, x_words, x_scales, w1, w2_words, w2_sca
                     nc.vector.tensor_scalar_max(out=h[t][:, j0 : j0 + n], in0=h_acc[(t, j0)][:, 0:n], scalar1=0.0)
                 else:
                     nc.scalar.activation(out=h[t][:, j0 : j0 + n], in_=h_acc[(t, j0)][:, 0:n], func=RELU)
-
-        share_added = sb([P, ADDED], F32, "share_added", "xg0")
-        nc.sync.dma_start(out=share_added[:], in_=share[:, TURNED:S])
 
         def gather(t, j0, j1, share_sb, dst):
             nc.vector.tensor_tensor(
@@ -227,7 +225,7 @@ def tile_picked_treeup_relu_p_kernel(tc, x_words, x_scales, w1, w2_words, w2_sca
                     for s in range(2):
                         turn(z_t[g], 2 * s + e, h[2 * u + e], 2 * g + s, start=(e == 0 and s == 0))
             for e in range(2):
-                gather(2 * u + e, 0, TURNED, share_turned[:], taken[:, 2 * u + e, :])
+                gather(2 * u + e, 0, TURNED, share_turned, taken[:, 2 * u + e, :])
                 for g in range(2):
                     for s in range(2):
                         turn(z_t[g], 2 * s + e, taken[:, 2 * u + e, :], 2 * g + s, stop=(e == 1 and s == 1))
@@ -263,7 +261,7 @@ def tile_picked_treeup_relu_p_kernel(tc, x_words, x_scales, w1, w2_words, w2_sca
                 op=MULT,
             )
 
-        gather(PACK - 1, TURNED, S, share_added[:], taken_added[:, PACK - 1, :])
+        gather(PACK - 1, TURNED, S, share_added, taken_added[:, PACK - 1, :])
         weigh(0, PAIR, FETCHED)
         weigh(PAIR, ADDED - PAIR, FETCHED)
 
@@ -289,15 +287,15 @@ def tile_picked_treeup_relu_p_kernel(tc, x_words, x_scales, w1, w2_words, w2_sca
                 stop=True,
             )
 
-        def store(acc, j0, n, copy):
-            res = sb([P, n], F32, "res%d" % j0)
-            copy(out=res[:], in_=acc)
-            nc.sync.dma_start(out=out[:, j0 : j0 + n], in_=res[:])
+        res = sb([P, S], F32, "res")
+
+        def store(j0, n):
+            nc.sync.dma_start(out=out[:, j0 : j0 + n], in_=res[:, j0 : j0 + n])
 
         def finish(z_in, j0, n, b):
             acc = bank(b, "oacc%d" % j0)
             product(z_in, j0, n, acc[:, 0:n], sb([P, n], U32, "zc%d" % j0))
-            store(acc[:, 0:n], j0, n, nc.scalar.copy)
+            nc.scalar.copy(out=res[:, j0 : j0 + n], in_=acc[:, 0:n])
 
         z_added = [sb([P, BLK * PACK], BF16, "z_added%d" % b) for b in range(2)]
         for b in range(2):
@@ -305,12 +303,21 @@ def tile_picked_treeup_relu_p_kernel(tc, x_words, x_scales, w1, w2_words, w2_sca
         finish(z_added[0][:], TURNED, BLK, 6)
         for g in range(2):
             finish(z_pairs[:, g * PAIR * PACK : (g + 1) * PAIR * PACK], g * PAIR, PAIR, g)
+            store(g * PAIR, PAIR)
         finish(z_last[:], last * BLK, BLK, 2)
+        store(2 * PAIR, PAIR)
         z_end = placed([P, BLK * PACK], BF16, "z_end", 0)
         add(z_end[:], PAIR, BLK)
-        accs = [bank(3 + b, "oacc_end%d" % b) for b in range(2)]
         behind_z_end = 2 * BLK * PACK
-        product(z_added[1][:], TURNED + BLK, BLK, accs[0][:, 0:BLK], placed([P, BLK], U32, "zc_late", behind_z_end))
-        product(z_end[:], TURNED + PAIR, BLK, accs[1][:, 0:BLK], sb([P, BLK], U32, "zc_end"))
+        end = TURNED + PAIR
+        acc = bank(3, "oacc_late")
+        product(z_added[1][:], TURNED + BLK, BLK, acc[:, 0:BLK], placed([P, BLK], U32, "zc_late", behind_z_end))
+        nc.scalar.copy(out=res[:, end - BLK : end], in_=acc[:, 0:BLK])
+        store(end - BLK, BLK)
         for b, copy in enumerate((nc.scalar.copy, nc.vector.tensor_copy)):
-            store(accs[b][:, 0:BLK], TURNED + (1 + b) * BLK, BLK, copy)
+            j0 = end + b * HALF
+            acc = bank(4 + b, "oacc_end%d" % b)
+            z_in = z_end[:, b * HALF * PACK : (b + 1) * HALF * PACK]
+            product(z_in, j0, HALF, acc[:, 0:HALF], sb([P, HALF], U32, "zc_end%d" % b))
+            copy(out=res[:, j0 : j0 + HALF], in_=acc[:, 0:HALF])
+        store(end, BLK)

@@ -301,11 +301,12 @@ def tile_picked_treeup_relu_p_kernel(tc, x_words, x_scales, w1, w2_words, w2_sca
         for b in range(2):
             add(z_added[b][:], b * BLK, BLK)
         finish(z_added[0][:], TURNED, BLK, 6)
+        store(TURNED, BLK)
         for g in range(2):
             finish(z_pairs[:, g * PAIR * PACK : (g + 1) * PAIR * PACK], g * PAIR, PAIR, g)
             store(g * PAIR, PAIR)
         finish(z_last[:], last * BLK, BLK, 2)
-        store(2 * PAIR, PAIR)
+        store(last * BLK, BLK)
         z_end = placed([P, BLK * PACK], BF16, "z_end", 0)
         add(z_end[:], PAIR, BLK)
         behind_z_end = 2 * BLK * PACK

@@ -115,7 +115,7 @@ def tile_picked_treeup_relu_p_kernel(tc, x_words, x_scales, w1, w2_words, w2_sca
                 w1_mx[(z, t0 + i)] = (codes[:, i * P : (i + 1) * P], scales[:, i * P : (i + 1) * P])
 
         xg = [sb([P, S], U32, "xg%d" % z) for z in range(PASSES)]
-        spans = [[(4 * (1 - t) + a, a * PAIR, PAIR) for a in range(4)] for t in range(2)]
+        spans = [[(4 + a, a * PAIR, PAIR) for a in range(4)], [(a, a * BANK, BANK) for a in range(2)]]
         spans = spans + [[(2 * t + a, a * BANK, BANK) for a in range(2)] for t in range(2, PACK)]
         h_acc = {}
 

from contextlib import ExitStack

import concourse.mybir as mybir
from concourse.masks import make_identity

K, T, S, H, N = 1024, 2048, 1024, 512, 128
FLOPS = 2 * K * H * S + 2 * H * N * S

F32 = mybir.dt.float32
BF16 = mybir.dt.bfloat16
I32 = mybir.dt.int32
U32 = mybir.dt.uint32
U16 = mybir.dt.uint16
U8 = mybir.dt.uint8
FP8X4 = mybir.dt.float8_e4m3fn_x4
MULT = mybir.AluOpType.mult
ADD = mybir.AluOpType.add
RELU = mybir.ActivationFunctionType.Relu
COPY = mybir.ActivationFunctionType.Copy

P = 128
PACK = 4
PASSES = K // (P * PACK)
BANK = 512
BLK = 128
ROWS = 16
PAIR = 2 * BLK
HALF = P // 2
TURNED = 5 * BLK
ADDED = S - TURNED
FETCHED = 3
SPREAD = 4
FREED = 8192


def tile_picked_treeup_relu_p_kernel(tc, x_words, x_scales, w1, w2_words, w2_scales, share, offs, par, out):
    nc = tc.nc
    with ExitStack() as ctx:
        keep = ctx.enter_context(tc.tile_pool(name="keep", bufs=1))
        late = ctx.enter_context(tc.tile_pool(name="late", bufs=1))
        psum = ctx.enter_context(tc.psum_pool(name="psum", bufs=1))

        def sb(shape, dtype, name, reuses=None):
            return keep.tile(shape, dtype, name=name, tag=reuses or name, align_bytes=256)

        def placed(shape, dtype, name, offset):
            return late.tile(shape, dtype, name=name, offset=offset, align_bytes=256)

        def bank(b, name):
            return psum.tile([P, BANK], F32, name=name, tag="bank%d" % b)

        offs_sb = keep.tile([P, S // ROWS], U16, name="offs_sb")
        par_sb = keep.tile([P, S // ROWS], U16, name="par_sb")
        xw = [placed([P, T], U32, "xw0", FREED), sb([P, T], U32, "xw1")]
        xs = sb([P, T], U8, "xs")
        xsg = sb([P, S], U8, "xsg")
        planes = sb([P, PASSES, S], U8, "planes")
        w1_raw = [sb([P, PACK, H], F32, "w1raw0")]
        zeros = sb([P, P], F32, "zeros")
        ident = sb([P, P], F32, "ident")

        nc.gpsimd.memset(xs[:].bitcast(I32), 0)
        nc.gpsimd.memset(zeros[:], 0.0)
        nc.scalar.copy(out=ident[:], in_=zeros[:])
        nc.gpsimd.memset(planes[:].rearrange("p z s -> p (z s)").bitcast(I32), 0)
        make_identity(nc, ident[:], nomemset=True)

        def load_x(z):
            nc.sync.dma_start(out=xw[z][:].bitcast(I32), in_=x_words[z].rearrange("p c r -> p (c r)").bitcast(I32))

        def load_w1(z, j0, j1):
            rows = w1[z * P * PACK : (z + 1) * P * PACK, :].rearrange("(p j) c -> p j c", j=PACK)
            nc.sync.dma_start(out=w1_raw[z][:, j0:j1, :], in_=rows[:, j0:j1, :])

        def move_scales(z):
            for q in (0, 2, 1, 3):
                first = SPREAD * (16 * z + 4 * q)
                nc.sync.dma_start(
                    out=planes[32 * q + 4 * z : 32 * q + 4 * z + 4, z, :].bitcast(I32),
                    in_=xsg[first : first + 4 * SPREAD : SPREAD, :].bitcast(I32),
                )

        load_w1(0, 0, 1)
        nc.sync.dma_start(offs_sb[:], offs)
        nc.sync.dma_start(
            out=xs[0 : 32 * SPREAD : SPREAD, :].bitcast(I32), in_=x_scales.rearrange("z q c -> (z q) c").bitcast(I32)
        )
        load_x(0)
        load_w1(0, 1, PACK)
        load_x(1)
        nc.sync.dma_start(par_sb[:], par)
        nc.vector.tensor_copy(out=xsg[:], in_=xs[:].indirect(offs_sb[:]))
        move_scales(0)
        w1_raw.append(sb([P, PACK, H], F32, "w1raw1", "xs"))
        load_w1(1, 0, PACK)
        move_scales(1)

        w1_bf = {(z, u): sb([P, 2, P, PACK], BF16, "w1bf%d%d" % (z, u)) for z in range(PASSES) for u in range(2)}
        w1_mx = {}

        def cast_w1(copy, z, u, m0, m1):
            src = w1_raw[z][:].rearrange("p j (m t) -> p m j t", t=PACK)[:, m0:m1, :, 2 * u : 2 * u + 2]
            copy(out=w1_bf[(z, u)][:].rearrange("p e m j -> p m j e")[:, m0:m1], in_=src)

        def quant_w1(z, t0, planes, reuses=None):
            u, e = divmod(t0, 2)
            codes = sb([P, planes * P], U32, "w1c%d%d" % (z, t0), reuses)
            scales = sb([P, planes * P], U8, "w1s%d%d" % (z, t0))
            nc.vector.quantize_mx(
                out=codes[:].bitcast(FP8X4),
                scales=scales[:],
                in_=w1_bf[(z, u)][:, e : e + planes].rearrange("p e m j -> p (e m j)"),
            )
            for i in range(planes):
                w1_mx[(z, t0 + i)] = (codes[:, i * P : (i + 1) * P], scales[:, i * P : (i + 1) * P])

        xg = [sb([P, S], U32, "xg%d" % z) for z in range(PASSES)]
        spans = [[(4 + a, a * PAIR, PAIR) for a in range(4)], [(a, a * BANK, BANK) for a in range(2)]]
        spans = spans + [[(2 * t + a, a * BANK, BANK) for a in range(2)] for t in range(2, PACK)]
        h_acc = {}

        def first_product(z, t):
            codes, scales = w1_mx[(z, t)]
            for b, j0, n in spans[t]:
                if z == 0:
                    h_acc[(t, j0)] = bank(b, "hacc%d_%d" % (t, j0))
                nc.tensor.matmul_mx(
                    out=h_acc[(t, j0)][:, 0:n],
                    lhsT=codes.bitcast(FP8X4),
                    lhsT_scale=scales,
                    rhs=xg[z][:, j0 : j0 + n].bitcast(FP8X4),
                    rhs_scale=planes[4 * z : P, z, j0 : j0 + n],
                    start=(z == 0),
                    stop=(z == PASSES - 1),
                )

        nc.vector.tensor_copy(out=xg[0][:], in_=xw[0][:].indirect(offs_sb[:]))
        cast_w1(nc.scalar.copy, 0, 0, 0, P)
        cast_w1(nc.scalar.copy, 0, 1, 0, P // 4)
        cast_w1(nc.vector.tensor_copy, 0, 1, P // 4, P)
        for u in range(2):
            quant_w1(0, 2 * u, 2)
        nc.vector.tensor_copy(out=xg[1][:], in_=xw[1][:].indirect(offs_sb[:]))
        share_sb = placed([P, S], F32, "share_sb", FREED)
        share_turned, share_added = share_sb[:, 0:TURNED], share_sb[:, TURNED:S]
        w2w = placed([P, N], U32, "w2w", FREED + 4 * S)
        w2s = placed([P, N], U8, "w2s", FREED + 4 * S + 4 * N)
        nc.sync.dma_start(out=share_sb[:], in_=share)
        nc.sync.dma_start(out=w2w[:].bitcast(I32), in_=w2_words[0].rearrange("p c r -> p (c r)").bitcast(I32))
        nc.gpsimd.memset(w2s[:].bitcast(I32), 0)
        for q in range(4):
            nc.sync.dma_start(
                out=w2s[32 * q : 32 * q + 4, :].bitcast(I32),
                in_=w2_scales[0, 4 * q : 4 * q + 4, :].bitcast(I32),
            )
        for t in range(2):
            first_product(0, t)
        for u in range(2):
            cast_w1(nc.scalar.copy, 1, u, 0, HALF)
            cast_w1(nc.vector.tensor_copy, 1, u, HALF, P)
        quant_w1(1, 0, 1)
        quant_w1(1, 1, 1)
        quant_w1(1, 2, 2)

        h = [sb([P, S], F32, "h%d" % t) for t in range(PACK)]
        for t in range(PACK):
            if t >= 2:
                first_product(0, t)
            first_product(1, t)
            for i, (b, j0, n) in enumerate(spans[t]):
                if t == 0 and i in (1, 2):
                    nc.vector.tensor_scalar_max(out=h[t][:, j0 : j0 + n], in0=h_acc[(t, j0)][:, 0:n], scalar1=0.0)
                else:
                    nc.scalar.activation(out=h[t][:, j0 : j0 + n], in_=h_acc[(t, j0)][:, 0:n], func=RELU)

        def gather(t, j0, j1, share_sb, dst):
            nc.vector.tensor_tensor(
                out=dst, in0=h[t][:].indirect(par_sb[:, j0 // ROWS : j1 // ROWS]), in1=share_sb, op=MULT
            )

        fetched = sb([P, FETCHED, ADDED], F32, "fetched")
        for t in range(FETCHED):
            nc.scalar.activation(
                out=fetched[:, t, :], in_=h[t][:].indirect(par_sb[:, TURNED // ROWS : S // ROWS]), func=COPY
            )

        def turn(z_t, slot, src, b, start=False, stop=False):
            nc.tensor.matmul(
                out=z_t[:, slot * P : (slot + 1) * P],
                lhsT=src[:, b * BLK : (b + 1) * BLK],
                rhs=ident[:],
                start=start,
                stop=stop,
                is_transpose=True,
            )

        def round_rows(z_t, name):
            z_rows = sb([P, BANK], BF16, name)
            nc.scalar.copy(
                out=z_rows[:].rearrange("p (s m e) -> p s m e", m=P, e=2),
                in_=z_t[:].rearrange("p (s e m) -> p s m e", m=P, e=2),
            )
            return z_rows

        def turn_back(z_rows, back, slots):
            words = z_rows[:].bitcast(F32)
            for s, slot in enumerate(slots):
                nc.tensor.transpose(back[:, slot * P : (slot + 1) * P], words[:, s * P : (s + 1) * P], ident[:])

        def lay_out(z_in, back, blocks):
            nc.scalar.copy(
                out=z_in.bitcast(F32).rearrange("p (s j u) -> p s j u", j=BLK, u=2),
                in_=back[:, 0 : 2 * blocks * P].rearrange("p (s u j) -> p s j u", j=BLK, u=2),
            )

        taken = sb([P, PACK, TURNED], F32, "taken_turned")
        back = [bank(6 + g, "back%d" % g) for g in range(2)]
        last = TURNED // BLK - 1
        zt_last = bank(4, "zt_last")
        rows = []
        for u in range(2):
            z_t = [bank(2 * u + g, "zt%d%d" % (g, u)) for g in range(2)]
            for e in range(2):
                for g in range(2):
                    for s in range(2):
                        turn(z_t[g], 2 * s + e, h[2 * u + e], 2 * g + s, start=(e == 0 and s == 0))
            for e in range(2):
                gather(2 * u + e, 0, TURNED, share_turned, taken[:, 2 * u + e, :])
                for g in range(2):
                    for s in range(2):
                        turn(z_t[g], 2 * s + e, taken[:, 2 * u + e, :], 2 * g + s, stop=(e == 1 and s == 1))
            if u == 1:
                for t in range(PACK):
                    turn(zt_last, t, h[t], last, start=(t == 0))
                for t in range(PACK):
                    turn(zt_last, t, taken[:, t, :], last, stop=(t == PACK - 1))
                for g in range(2):
                    turn_back(rows[g], back[g], (0, 2))
            rows = [round_rows(z_t[g], "zrows%d%d" % (g, u)) for g in range(2)]
        for g in range(2):
            turn_back(rows[g], back[g], (1, 3))

        back_last = bank(5, "back_last")
        turn_back(round_rows(zt_last, "zrows_last"), back_last, (0, 1))
        z_pairs = placed([P, 2 * PAIR * PACK], BF16, "z_pairs", 0)
        for g in range(2):
            lay_out(z_pairs[:, g * PAIR * PACK : (g + 1) * PAIR * PACK], back[g], 2)
        z_last = sb([P, BLK * PACK], BF16, "z_last")
        lay_out(z_last[:], back_last, 1)

        own = sb([P, PACK, ADDED], F32, "own")
        for t in range(PACK):
            nc.sync.dma_start(out=own[:, t, :], in_=h[t][:, TURNED:S])
        taken_added = sb([P, PACK, ADDED], F32, "taken_added")

        def weigh(j0, n, planes):
            nc.vector.tensor_tensor(
                out=taken_added[:, 0:planes, j0 : j0 + n],
                in0=fetched[:, 0:planes, j0 : j0 + n],
                in1=share_added[:, j0 : j0 + n].unsqueeze(1).to_broadcast([P, planes, n]),
                op=MULT,
            )

        gather(PACK - 1, TURNED, S, share_added, taken_added[:, PACK - 1, :])
        weigh(0, PAIR, FETCHED)
        weigh(PAIR, ADDED - PAIR, FETCHED)

        def add(z_in, j0, n):
            cols = slice(j0, j0 + n)
            nc.vector.tensor_tensor(
                out=z_in.rearrange("p (c i t) -> p c t i", i=4, t=PACK),
                in0=own[:, :, cols].rearrange("p t (c i) -> p c t i", i=4),
                in1=taken_added[:, :, cols].rearrange("p t (c i) -> p c t i", i=4),
                op=ADD,
            )

        def product(z_in, j0, n, acc, codes):
            scales = sb([P, n], U8, "zs%d" % j0)
            nc.vector.quantize_mx(out=codes[:].bitcast(FP8X4), scales=scales[:], in_=z_in)
            nc.tensor.matmul_mx(
                out=acc,
                lhsT=w2w[:].bitcast(FP8X4),
                lhsT_scale=w2s[:],
                rhs=codes[:].bitcast(FP8X4),
                rhs_scale=scales[:],
                start=True,
                stop=True,
            )

        res = sb([P, S], F32, "res")

        def store(j0, n):
            nc.sync.dma_start(out=out[:, j0 : j0 + n], in_=res[:, j0 : j0 + n])

        def finish(z_in, j0, n, b):
            acc = bank(b, "oacc%d" % j0)
            product(z_in, j0, n, acc[:, 0:n], sb([P, n], U32, "zc%d" % j0))
            nc.scalar.copy(out=res[:, j0 : j0 + n], in_=acc[:, 0:n])

        z_added = [sb([P, BLK * PACK], BF16, "z_added%d" % b) for b in range(2)]
        for b in range(2):
            add(z_added[b][:], b * BLK, BLK)
        finish(z_added[0][:], TURNED, BLK, 6)
        store(TURNED, BLK)
        for g in range(2):
            finish(z_pairs[:, g * PAIR * PACK : (g + 1) * PAIR * PACK], g * PAIR, PAIR, g)
            store(g * PAIR, PAIR)
        finish(z_last[:], last * BLK, BLK, 2)
        store(last * BLK, BLK)
        z_end = placed([P, BLK * PACK], BF16, "z_end", 0)
        add(z_end[:], PAIR, BLK)
        behind_z_end = 2 * BLK * PACK
        end = TURNED + PAIR
        acc = bank(3, "oacc_late")
        product(z_added[1][:], TURNED + BLK, BLK, acc[:, 0:BLK], placed([P, BLK], U32, "zc_late", behind_z_end))
        nc.scalar.copy(out=res[:, end - BLK : end], in_=acc[:, 0:BLK])
        store(end - BLK, BLK)
        for b, copy in enumerate((nc.scalar.copy, nc.vector.tensor_copy)):
            j0 = end + b * HALF
            acc = bank(4 + b, "oacc_end%d" % b)
            z_in = z_end[:, b * HALF * PACK : (b + 1) * HALF * PACK]
            product(z_in, j0, HALF, acc[:, 0:HALF], sb([P, HALF], U32, "zc_end%d" % b))
            copy(out=res[:, j0 : j0 + HALF], in_=acc[:, 0:HALF])
        store(end, BLK)
